import numpy as np, ml_dtypes
CORES = [5,29,101,125,133,157,229,253]
N = 8
import mx_ref
BF = ml_dtypes.bfloat16
def gentries(a):
    return np.ascontiguousarray(a.reshape(8, 16, -1).transpose(0, 2, 1)).reshape(8, -1)
def gtable(e):
    e = np.asarray(e); return np.ascontiguousarray(e.reshape(8, -1, 16).transpose(0, 2, 1)).reshape(128, -1).astype(np.int32)
def gcols(t, e):
    v = np.concatenate([t.reshape(8, 16, -1, 4), np.zeros((8, 16, 1, 4), BF)], axis=2)
    return np.ascontiguousarray(np.stack([v[g][:, e[g]] for g in range(8)])).reshape(128, -1)
def tile(rs):
    return np.stack(rs, axis=2).reshape(128, -1).astype(BF)
def pick(q, e):
    c = np.concatenate([q[0].reshape(128, -1, 4), np.zeros((128, 1, 4), np.uint8)], axis=1); s = np.concatenate([q[1], np.ones((16, 1), np.uint8)], axis=1)
    return (np.ascontiguousarray(c[:, e].reshape(128, -1)), np.ascontiguousarray(s[:, e]))
def join(*qs):
    return (np.concatenate([q[0] for q in qs], axis=1), np.concatenate([q[1] for q in qs], axis=1))
def put(q, e, v):
    c, s = q[0].reshape(128, -1, 4).copy(), q[1].copy(); c[:, e] = v[0].reshape(128, -1, 4); s[:, e] = v[1]
    return (c.reshape(128, -1), s)
def pk(c, s):
    return (np.ascontiguousarray(c), mx_ref.live(s))
def emit(q):
    return q[0], q[1]
def packed(v, rng):
    q = [mx_ref.quantize(np.ascontiguousarray(v[r])) for r in range(N)]
    return np.stack([a for a, b in q]), np.stack([mx_ref.plane(b, rng) for a, b in q])
def values_of_codes():
    e, c = np.zeros((128, 128, 4), np.float32), np.zeros((128, 2, 4), np.uint8)
    e[np.arange(128), np.arange(128), 0] = 1
    c[:127, :, 0] = np.arange(256).reshape(2, 128).T[:127]
    return mx_ref.matmul(mx_ref.quantize(e.reshape(128, 512).astype(BF)), (c.reshape(128, 8), np.full((16, 2), 127, np.uint8))).T.reshape(-1).astype(np.float64)
CODE_VALUE, SCALE_VALUE = values_of_codes(), 2.0 ** (np.arange(256) - 127.0)
def decode(q):
    return (CODE_VALUE[q[0]].reshape(16, 8, -1, 4) * SCALE_VALUE[q[1]][:, None, :, None] + 0.0).reshape(128, -1).astype(np.float32)
def f(rng, *shape):
    return mx_ref.flush((rng.standard_normal(shape, dtype=np.float32) * np.exp2(rng.integers(-2, 3, shape[:-1] + (1,)))).astype(BF))
def wide(rng, *shape, cols=0):
    v = rng.standard_normal(shape, dtype=np.float32) * np.exp2(rng.integers(-12, 13, shape)).astype(np.float32)
    if cols: v *= np.repeat(np.exp2(rng.integers(-cols, cols + 1, shape[:-2] + (1, shape[-1] // 4))) * (rng.random(shape[:-2] + (1, shape[-1] // 4)) > 0.0625), 4, axis=-1).astype(np.float32)
    return mx_ref.flush(v.astype(BF))
C, H = 288, 144
MASK = [4, 1, 2]
def numbers_of(rng):
    return {"x": np.array(f(rng, N, 128, 4 * C)), "u": np.array(f(rng, N, 128, 512)), "v": np.array(f(rng, N, 128, 512))}
def stored(l, k):
    return {"gl": np.stack([gtable(l[r]) for r in range(N)]), "gk": np.stack([gtable(k[r]) for r in range(N)])}
def lists(rng):
    e = np.tile(np.arange(C), (N, 8, 1))
    return stored(rng.permuted(e, axis=2), rng.permuted(e, axis=2))
def layers(rng, still=[]):
    w = np.array(f(rng, N, 128, 2048)).reshape(N, 8, 16, 4, 8, 16, 4)
    for i in still:
        w[:, :, i] = 0
        w[:, :, :, :, :, i] = 0
    return w
def weights(rng, w):
    c, p = packed(np.ascontiguousarray(w).reshape(N, 128, 2048), rng)
    return {"wc": c, "ws": p}
def setup_inputs(rng):
    return {**numbers_of(rng), **lists(rng), **weights(rng, layers(rng))}
def setup_inputs_ties(rng):
    d = numbers_of(rng)
    o = rng.permutation(N)
    k = rng.integers(-1, 2, (N, 8, C, 2)).astype(np.float32)
    k[o[1]] = 1
    k[o[2]] = -1
    x = d["x"].reshape(N, 8, 16, C, 4)
    x[:, :, 0] = 0
    x[:, :, 0, :, :2] = k.astype(BF)
    a = np.exp2(rng.integers(-3, 4, 8).astype(np.float32))[None, :, None]
    x[:, :, 8:] = 0
    x[:, :, 8, :, 0] = (-1.125 * a).astype(BF)
    x[:, :, 10, :, 0] = (-0.0703125 * a).astype(BF)
    c = np.ones(N, np.float32)
    c[o[0]] = 0
    u = d["u"].reshape(N, 128, 128, 4)
    for t in range(2):
        u[:, :, t::16] = 0
        for h in range(0, 128, 16): u[:, h, h + t, t] = c.astype(BF)
    w = layers(rng, [0])
    w[:, :, :, :, :, 8:] = 0
    for g in range(8):
        w[:, g, 8, 0, g, 8, 0] = -28.0
        for b in range(4): w[:, g, 10, b, g, 9, 0] = -2.0 ** (b - 5)
    return {"x": x.reshape(N, 128, 4 * C), "u": u.reshape(N, 128, 512), "v": d["v"], **stored(rng.integers(0, C, (N, 8, C)), rng.integers(0, C, (N, 8, C))), **weights(rng, w)}
def setup_inputs_near(rng):
    d = numbers_of(rng)
    o = rng.permutation(N) % 2
    k = np.where(o == 0, 2.0 ** -30, 1.0).astype(np.float32)
    x = d["x"].astype(np.float32).reshape(N, 8, 16, C, 4)
    x[:, :, :8] = 0
    s = rng.integers(-1, 2, (N, 8, C, 2)) * k[:, None, None, None]
    x[:, :, 0, :, :2] = 1.125 * s
    x[:, :, 1, :, :2] = -1.25 * s
    x[:, :, 3, :, :2] = rng.choice([-1.0, 1.0], (N, 8, C, 2)) * 2.0 ** -30
    x[:, :, 5] = 2.0 ** -30
    for r in range(N):
        for g in rng.permutation(8)[:4]: x[r, g, 0, rng.integers(C), 0] = 2.0 ** 30 * rng.choice([-1.0, 1.0])
    u = d["u"].reshape(N, 128, 128, 4)
    w = layers(rng, range(8))
    for t in range(2):
        u[:, :, t::16] = 0
        for h in range(0, 128, 16):
            u[:, h, h + t, t] = (1.125 * k).astype(BF)
            u[:, h + 1, h + t, t] = k.astype(BF)
            u[:, h + 2, h + t, t] = k.astype(BF)
        for g in range(8):
            w[:, g, 3, t, g, 2, t] = 2.0 ** -8
            w[:, g, 3, t, g, 4, t] = 32.0
    return {"x": x.reshape(N, 128, 4 * C).astype(BF), "u": u.reshape(N, 128, 512), "v": d["v"], **lists(rng), **weights(rng, w)}
def setup_inputs_odd(rng):
    d = numbers_of(rng)
    x = (1.0 + (2 * rng.integers(0, 64, (N, 16, 8, C, 4)) + 1) * 2.0 ** -7) * np.exp2(-rng.integers(0, 7, (N, 16, 8, C, 4)).astype(np.float64)) * rng.choice([-1.0, 1.0], (N, 16, 8, C, 4))
    x[:, :, 0, :, 0] = 1.96875 * 2.0 ** 8 * rng.choice([-1.0, 1.0], (N, 16, C))
    x[:, ::2, 1, :, :2] = rng.integers(7, 10, (N, 8, C, 2)) * 2.0 ** -8
    x[:, ::2, 2, :, :2] = 2.0 ** -5
    u = d["u"].reshape(N, 16, 8, 128, 4)
    for t in range(2):
        u[:, :, :, t::16] = 0
        for g in range(8):
            u[:, 2 * g, 1, 16 * g + t, t] = 1.0
            u[:, 2 * g, 2, 16 * g + t, t] = -1.0
    return {"x": x.astype(np.float32).reshape(N, 128, 4 * C).astype(BF), "u": u.reshape(N, 128, 512), "v": d["v"], **lists(rng), **weights(rng, layers(rng, [0, 1, 2, 8]))}
def setup_inputs_ends(rng):
    d = numbers_of(rng)
    x = np.zeros((N, 128, C, 4))
    u = d["u"].astype(np.float32).reshape(N, 128, 128, 4)
    v = d["v"].astype(np.float32)
    w = np.zeros((N, 128, 4, 128, 4), np.float32)
    o, e = rng.permutation(N) % 4, rng.permutation(N) % 4
    i = np.arange(128)
    def amount(large, *n):
        return (0.9 + 0.1 * rng.random(n)) * 2.0 ** 30 if large else (1.0 + 0.125 * rng.integers(0, 8, n)) * 2.0 ** -30
    for r in range(N):
        large = o[r] < 2
        if o[r] == 3: x[r] = d["x"][r].astype(np.float32).reshape(128, C, 4)[:, :1]
        else: x[r] = -amount(large, 128, C, 4) * (0.5 if large else 1.0)
        if o[r] == 1: x[r] *= rng.choice([-1.0, 1.0], (1, C, 1))
        x[r, 7::8] = 2.0 ** -30
        for t in range(2):
            h = rng.permutation(8)
            c = np.where(h < 2, 0.0, h % 2 * 2.0 - 1.0)[None, :, None]
            if o[r] == 3: u[r, :, t::16] *= np.abs(c).astype(np.float32)
            else: u[r, :, t::16] = c * amount(large, 128, 8, 4)
        v[r] = rng.choice([-1.0, 1.0], (128, 512)) * amount(large, 128, 512)
        k = np.array([1.0, 2.0, 4.0])[rng.permutation(8) % 3][i // 16]
        k[7::8] = 0
        if o[r] == 2: k = np.where(i % 8 == 7, 2.0 ** 8, 2.0 ** -8)
        for b in range(4): w[r, i, b, i, b] = k
    both = []
    for z in (e, (e + rng.integers(1, 4)) % 4):
        a = rng.integers(0, C, (N, 8, C))
        a[z == 0] = C - 1
        a[z == 1] = 0
        a[z == 2] = rng.integers(0, 2, a[z == 2].shape) * (C - 1)
        both.append(a)
    return {"x": x.astype(np.float32).reshape(N, 128, 4 * C).astype(BF), "u": u.reshape(N, 128, 512).astype(BF), "v": v.astype(BF), **stored(*both), **weights(rng, w.astype(BF))}
def setup_inputs_spread(rng):
    d = setup_inputs(rng)
    d["x"] = wide(rng, N, 128, 4 * C, cols=6)
    return d
def check_inputs(d):
    b = []
    for k in ("x", "u", "v"):
        a = np.abs(d[k].astype(np.float32))
        if not (np.isfinite(a).all() and ((a == 0) | (a >= 2.0 ** -30) & (a <= 2.0 ** 30)).all()): b.append("a value of " + k)
    for k in ("gl", "gk"):
        if not ((d[k] >= 0) & (d[k] < C)).all(): b.append("an entry of " + k)
    none, least, most = [emit(mx_ref.quantize(np.full((128, 16), k, np.float32).astype(BF)))[1][0, 0] for k in (0.0, 2.0 ** -8, 2.0 ** 8)]
    for r in range(N):
        if ((d["wc"][r] == 0x7F) | (d["wc"][r] == 0xFF)).any(): b.append("wc: a code that is no number")
        s = mx_ref.live(d["ws"][r])
        if ((s != none) & ((s < least) | (s > most))).any(): b.append("ws: a scale out of range")
        if (((d["wc"][r].reshape(16, 8, 512, 4) & 0x7F) != 0) & (s == none)[:, None, :, None]).any(): b.append("wc: a code other than zero under the scale of zeros")
    return b
def at(t, e):
    return np.take_along_axis(t, e, axis=1)
def reference(x, u, v, gl, gk, wc, ws):
    qu = [mx_ref.quantize(u[r]) for r in range(N)]
    lay = [pk(wc[r], ws[r]) for r in range(N)]
    left, right = [gentries(gl[r]) for r in range(N)], [gentries(gk[r]) for r in range(N)]
    now = [x[r] for r in range(N)]
    for mask in MASK:
        point, made, sent, turn = [], [], [], []
        for r in range(N):
            l, k = left[r], right[r]
            s = mx_ref.matmul(qu[r], mx_ref.quantize(now[r]))
            b = s[::16] > 0
            turn.append(s[1::16][:, :H] < 0)
            state, down = b, []
            for t in range(3):
                a, c = at(state, l), at(state, k)
                down.append(np.where(a, l, np.where(c, k, np.arange(C))))
                state = b ^ (a & ~c)
            o = at(down[0], at(down[1], down[2]))
            z = (gcols(now[r], o).astype(np.float32) + gcols(now[r], at(l, o)).astype(np.float32)) * np.float32(0.5)
            q = mx_ref.quantize(z.astype(BF))
            h = tile([mx_ref.matmul(pick(lay[r], np.arange(128 * b, 128 * b + 128)), q) * np.float32(0.03125) for b in range(4)])
            point.append(o)
            made.append(h)
            sent.append(decode(mx_ref.quantize(h)).astype(BF))
        for r in range(N):
            p = r ^ mask
            l, k = left[r], right[r]
            m = at(point[p], k)
            add = np.concatenate([gcols(sent[p], m[:, :H]), gcols(made[r], m[:, H:])], axis=1)
            now[r] = (now[r].astype(np.float32) + add.astype(np.float32)).astype(BF)
            t = np.concatenate([turn[r], turn[r]], axis=1)
            left[r] = np.where(t, np.roll(k, H, axis=1), l)
            right[r] = np.where(t, np.roll(l, H, axis=1), k)
    y, lr = np.zeros((N, 128, C), np.float32), np.zeros((N, 8, 2 * C), np.float32)
    oc, osc = np.zeros((N, 128, 4 * C), np.uint8), np.zeros((N, 16, C), np.uint8)
    for r in range(N):
        q = mx_ref.quantize(now[r])
        y[r] = mx_ref.matmul(mx_ref.quantize(v[r]), q)
        lr[r] = np.concatenate([left[r], right[r]], axis=1)
        oc[r], osc[r] = emit(q)
    return {"y": y, "lr": lr, "oc": oc, "osc": osc}

@@ -1,0 +1,406 @@
+from concourse.bass import DstId, RemoteDMATransfer
+from concourse.mybir import dt, AluOpType as A, ActivationFunctionType as F
+
+N, MASK = 8, [4, 1, 2]
+C, H, G = 288, 144, 4
+R = [0.5, 1.5, 4.5]
+ONE = 4096.0
+f32, b16, i32, u16, u8, q8 = "float32", "bfloat16", "int32", "uint16", "uint8", "float8_e4m3fn_x4"
+SCRATCH = {
+    "xt": ("sbuf", [128, 4 * C], b16), "ut": ("sbuf", [128, 512], b16), "vt": ("sbuf", [128, 512], b16),
+    "glt": ("sbuf", [128, 18], i32), "gkt": ("sbuf", [128, 18], i32),
+    "qw": ("sbuf", [128, 512], q8), "sw": ("sbuf", [128, 512], u8),
+    "qu": ("sbuf", [128, 128], q8), "su": ("sbuf", [128, 128], u8),
+    "qr": ("sbuf", [128, 256], q8), "sr": ("sbuf", [128, 256], u8),
+    "qv": ("sbuf", [128, 128], q8), "sv": ("sbuf", [128, 128], u8),
+    "qx": ("sbuf", [128, C], q8), "sx": ("sbuf", [128, C], u8),
+    "qz": ("sbuf", [128, C], q8), "sz": ("sbuf", [128, C], u8),
+    "qe": ("sbuf", [128, 512], q8), "se": ("sbuf", [128, 512], u8),
+    "eye": ("sbuf", [128, 128], b16), "et": ("sbuf", [128, 2048], b16),
+    "pi": ("sbuf", [128, 4], i32), "pa": ("sbuf", [128, 4], i32), "pf": ("sbuf", [128, 4], f32), "a4": ("sbuf", [128, 4], f32), "m4": ("sbuf", [128, 4], f32),
+    "c4": ("sbuf", [128, C], f32), "c16": ("sbuf", [128, H], f32), "labc": ("sbuf", [128, C], f32),
+    "mask4": ("sbuf", [128, C], f32), "mask16": ("sbuf", [128, H], f32), "rs4": ("sbuf", [128, C], f32), "rs16": ("sbuf", [128, H], f32),
+    "lab": ("sbuf", [128, C], f32), "ofi": ("sbuf", [128, 16], i32), "ofu": ("sbuf", [128, 16], u16),
+    "lk": ("sbuf", [128, 36], f32), "df": ("sbuf", [128, 18], f32), "tt": ("sbuf", [128, 18], f32), "dt2": ("sbuf", [128, 18], f32),
+    "lk2": ("sbuf", [128, 36], u16), "kf": ("sbuf", [128, 36], u16),
+    "xlo": ("sbuf", [128, 72], u16), "oo": ("sbuf", [128, 72], u16), "oi": ("sbuf", [128, 72], i32), "oa": ("sbuf", [128, 72], i32),
+    "mi": ("sbuf", [128, 72], i32), "ma": ("sbuf", [128, 72], i32),
+    "sg": ("sbuf", [128, C], f32), "v0": ("sbuf", [128, 2 * C], f32), "v1": ("sbuf", [128, 2 * C], f32), "v2": ("sbuf", [128, 2 * C], f32),
+    "i1": ("sbuf", [128, 2 * C], f32), "i2": ("sbuf", [128, 2 * C], f32), "g1": ("sbuf", [128, 2 * C], f32), "g2": ("sbuf", [128, 2 * C], f32),
+    "yy": ("sbuf", [128, C], f32), "kv": ("sbuf", [128, C], f32), "dd": ("sbuf", [128, C], f32), "mb": ("sbuf", [128, C], f32),
+    "mk": ("sbuf", [128, C], f32), "sc": ("sbuf", [128, C], f32), "mk2": ("sbuf", [128, C], f32), "sc2": ("sbuf", [128, C], f32),
+    "mt": ("sbuf", [128, H], f32), "st": ("sbuf", [128, H], f32),
+    "lrow": ("sbuf", [128, 2 * C], f32),
+    "zz": ("sbuf", [128, 4 * C], b16), "zt": ("sbuf", [128, 4 * C], b16), "ht": ("sbuf", [128, 4 * C], b16), "hs": ("sbuf", [128, 4 * H], b16),
+    "ys": ("sbuf", [128, C], f32),
+    "pb": ("psum", [128, 1024], f32), "pt": ("psum", [128, 512], f32), "pr": ("psum", [128, 2048], f32),
+}
+for _r in range(3):
+    SCRATCH["ks%d" % _r] = ("sbuf", [128, 18], u16)
+    SCRATCH["kin%d" % _r] = ("sbuf", [128, 18], u16)
+    SCRATCH["mm%d" % _r] = ("sbuf", [128, 72], u16)
+    SCRATCH["min%d" % _r] = ("sbuf", [128, 36], u16)
+    SCRATCH["qh%d" % _r] = ("sbuf", [128, H], q8)
+    SCRATCH["sh%d" % _r] = ("sbuf", [128, H], u8)
+    SCRATCH["qin%d" % _r] = ("sbuf", [128, H], q8)
+    SCRATCH["sin%d" % _r] = ("sbuf", [128, H], u8)
+SCRATCH["hq"] = ("sbuf", [128, H // 2], q8)
+SCRATCH["hsc"] = ("sbuf", [128, H // 2], u8)
+SCRATCH["hk"] = ("sbuf", [128, 18], u16)
+SCRATCH["hm"] = ("sbuf", [128, 36], u16)
+SEMAPHORES = ["cv", "cs", "ct", "cg", "sent", "out", "hq", "hs", "hk", "hm"] + ["%s%d" % (n, r) for n in ("ak", "am", "aq") for r in range(3)] \
+    + ["ld%d" % i for i in range(8)] + ["ga%d" % i for i in range(6)]
+
+
+def handers(topo, core, dst):
+    if topo.may_write(core, dst):
+        return None
+    return [c for c in topo.cores_of(core) if c != core and topo.die(c) == topo.die(core) and topo.may_write(c, dst)]
+
+
+def engines8(topo, src, dst):
+    e = topo.engines(src, dst)[:8]
+    return len(e), sum(1 << i for i in e)
+
+
+def send(g, T, topo, core, dst, out, in_, sem):
+    n, m = engines8(topo, core, dst)
+    rid, pid = topo.addr(dst, core)
+    g.remote_dma(out, in_, T.sem[sem], T.sem["sent"], pid, rid, m)
+    return n
+
+
+def hand_on(g, core, T, topo):
+    done = 0
+    for r, mask in enumerate(MASK):
+        for i, a in enumerate(T.cores):
+            b = T.cores[i ^ mask]
+            hs = handers(topo, a, b)
+            if hs is None or core not in hs:
+                continue
+            j = hs.index(core)
+            n = len(topo.engines(a, core)) // len(hs)
+            w, mw = H // len(hs), 36 // len(hs)
+            c0 = j * w
+            kw = 18 // len(hs)
+            g.wait_ge(T.sem["hk"], n)
+            done += send(g, T, topo, core, b, T["kin%d" % r][:, j * kw:j * kw + kw], T["hk"][:, 0:kw], "ak%d" % r)
+            g.wait_ge(T.sem["hm"], n)
+            done += send(g, T, topo, core, b, T["min%d" % r][:, j * mw:j * mw + mw], T["hm"][:, 0:mw], "am%d" % r)
+            g.wait_ge(T.sem["hq"], n)
+            done += send(g, T, topo, core, b, T["qin%d" % r][:, c0:c0 + w].bitcast(dt.uint8), T["hq"][:, 0:w].bitcast(dt.uint8), "aq%d" % r)
+            g.wait_ge(T.sem["hs"], n)
+            done += send(g, T, topo, core, b, T["sin%d" % r][:, c0:c0 + w], T["hsc"][:, 0:w], "aq%d" % r)
+    if done:
+        g.wait_ge(T.sem["sent"], done)
+
+
+def rank_program(g, core, T, topo):
+    rank = T.rank_of(core)
+    if rank is None:
+        hand_on(g, core, T, topo)
+        return
+    Q = {"v": g.vector, "s": g.scalar, "t": g.tensor, "g": g, "y": g.sync}
+    own_sem = {"v": "cv", "s": "cs", "t": "ct", "g": "cg"}
+    count, waited = {}, {q: {} for q in Q}
+    lastw, readers, known = {}, {}, {}
+
+    def need(q, tok):
+        sem, val, _ = tok
+        if waited[q].get(sem, 0) >= val:
+            return
+        Q[q].wait_ge(T.sem[sem], val)
+        waited[q][sem] = val
+        for s, n in known.get((sem, val), {}).items():
+            if waited[q].get(s, 0) < n:
+                waited[q][s] = n
+
+    def before(q, reads, writes):
+        toks = [lastw[k] for k in reads + writes if k in lastw]
+        toks += [t for k in writes for t in readers.get(k, []) if t[2] != q]
+        best = {}
+        for t in toks:
+            if t[0] not in best or best[t[0]][1] < t[1]:
+                best[t[0]] = t
+        for t in best.values():
+            need(q, t)
+
+    def after(q, ins, sem, inc, reads, writes):
+        if sem is None:
+            sem = own_sem[q]
+        ins.then_inc(T.sem[sem], inc)
+        count[sem] = count.get(sem, 0) + inc
+        tok = (sem, count[sem], q)
+        known[tok[:2]] = dict(waited[q])
+        for k in reads:
+            readers.setdefault(k, []).append(tok)
+        for k in writes:
+            lastw[k] = tok
+            readers[k] = []
+
+    def parts(keys):
+        return [k for key in keys for k in (["X0e%d" % b for b in range(4)] if key == "X0" else [key])]
+
+    def op(q, name, args, reads, writes, sem=None, inc=1, **kw):
+        reads, writes = parts(reads), parts(writes)
+        before(q, reads, writes)
+        e = Q[q]
+        fn = {"copy": lambda: e.tensor_copy(*args), "tt": lambda: e.tensor_tensor(*args), "ts": lambda: e.tensor_scalar(*args),
+              "scan": lambda: e.tensor_tensor_scan(*args), "quant": lambda: e.quantize_mx(*args), "memset": lambda: e.memset(*args),
+              "act": lambda: e.activation(*args, **kw), "mm": lambda: e.matmul_mx(*args, True, True), "iota": lambda: e.iota(*args, **kw),
+              "sel": lambda: e.affine_select(*args), "dma": lambda: e.dma_start(*args, **kw)}[name]
+        after(q, fn(), sem, inc, reads, writes)
+
+    def load(q, i, out, in_, key):
+        op(q, "dma", (out, in_), [], [key], sem="ld%d" % i, inc=16)
+
+    expect, done = {}, [0]
+
+    def arrives(sem, n, key):
+        expect[sem] = n
+        lastw[key] = (sem, n, "far")
+
+    def ship(r, kind, out, in_, width, sem, key):
+        before("g", [key], [])
+        dst = T.cores[rank ^ MASK[r]]
+        hs = handers(topo, core, dst)
+        if hs is None:
+            done[0] += send(g, T, topo, core, dst, out(slice(0, width)), in_(slice(0, width)), sem)
+            return
+        w, ts = width // len(hs), []
+        land = T[{"hs": "hsc"}.get(kind, kind)][:, 0:w]
+        if kind == "hq":
+            land = land.bitcast(dt.uint8)
+        for j, h in enumerate(hs):
+            es = topo.engines(core, h)
+            n = len(es) // len(hs)
+            rid, pid = topo.addr(h, core)
+            ts.append(RemoteDMATransfer(dst_ids=[DstId(rid=rid, pnc=pid)], dma_engine_mask=sum(1 << e for e in es[j * n:j * n + n]), remote_sem=T.sem[kind],
+                                        src=in_(slice(j * w, j * w + w)), dst=land))
+            done[0] += n
+        g.remote_dma_fused(ts, local_sem=T.sem["sent"])
+
+    for r in range(3):
+        p = T.cores[rank ^ MASK[r]]
+        hs = handers(topo, p, core)
+        n, _ = engines8(topo, p if hs is None else hs[0], core)
+        n *= 1 if hs is None else len(hs)
+        arrives("ak%d" % r, n, "kin%d" % r)
+        arrives("am%d" % r, n, "min%d" % r)
+        arrives("aq%d" % r, 2 * n, "qin%d" % r)
+
+    def send_k(r):
+        ship(r, "hk", lambda c: T["kin%d" % r][:, c], lambda c: T["ks%d" % r][:, c], 18, "ak%d" % r, "ks%d" % r)
+
+    def send_m(r):
+        ship(r, "hm", lambda c: T["min%d" % r][:, c], lambda c: T["mm%d" % r][:, c.start + 36:c.stop + 36], 36, "am%d" % r, "mm%d" % r)
+
+    def send_h(r):
+        ship(r, "hq", lambda c: T["qin%d" % r][:, c].bitcast(dt.uint8), lambda c: T["qh%d" % r][:, c].bitcast(dt.uint8), H, "aq%d" % r, "qh%d" % r)
+        ship(r, "hs", lambda c: T["sin%d" % r][:, c], lambda c: T["sh%d" % r][:, c], H, "aq%d" % r, "qh%d" % r)
+
+    imprecise = {"allow_small_or_imprecise_dtypes": True}
+    load("y", 0, T.gkt[:], T.gk[:], "gkt")
+    load("s", 1, T.glt[:], T.gl[:], "glt")
+    load("s", 2, T.ut[:], T.u[:], "ut")
+    load("y", 3, T.xt[:, 576:1152], T.x[:, 576:1152], "X1")
+    load("y", 4, T.xt[:, 0:576], T.x[:, 0:576], "X0")
+    load("y", 5, T.qw[:].bitcast(dt.uint8), T.wc[:], "qw")
+    load("y", 6, T.sw[:], T.ws[:], "sw")
+    load("y", 7, T.vt[:], T.v[:], "vt")
+    op("g", "iota", (T.pi[:], [[0, 4]], 0, 1), [], ["pi"])
+    op("g", "iota", (T.a4[:], [[1, 4]], 0, 0), [], ["a4"], **imprecise)
+    op("g", "iota", (T.ofi[:], [[1, 2], [16, 8]], 0, 0), [], ["ofi"])
+    op("g", "iota", (T.labc[:], [[4, C]], 0, 0), [], ["labc"], **imprecise)
+    op("g", "iota", (T.c4[:], [[0, 72], [1, 4]], 0, 0), [], ["c4"], **imprecise)
+    op("v", "memset", (T.eye[:], 1.0), [], ["eye"])
+    op("v", "memset", (T.v0[:, 0:2 * C:2], 0.0), [], ["v0z"])
+    op("v", "memset", (T.i1[:, 0:2 * C:2], 0.0), [], ["i1z"])
+    op("v", "memset", (T.i2[:, 0:2 * C:2], 0.0), [], ["i2z"])
+    op("v", "ts", (T.pa[:, 0:1], T.pi[:, 0:1], 15, None, A.bitwise_and), ["pi"], ["pa0"])
+    op("v", "ts", (T.pa[:, 1:2], T.pi[:, 1:2], 3, None, A.bitwise_and), ["pi"], ["pa1"])
+    op("v", "copy", (T.ofu[:], T.ofi[:]), ["ofi"], ["ofu"])
+    op("v", "ts", (T.pa[:, 2:3], T.pa[:, 0:1], 2, None, A.logical_shift_right), ["pa0"], ["pa2"])
+    op("v", "copy", (T.pf[:, 0:3], T.pa[:, 0:3]), ["pa0", "pa1", "pa2"], ["pf"])
+    op("v", "ts", (T.lab[:], T.labc[:], T.pf[:, 1:2], 1.0 / ONE, A.add, A.mult), ["labc", "pf"], ["lab"])
+    op("v", "copy", (T.ks0[:], T.gkt[:]), ["gkt"], ["ks0"])
+    send_k(0)
+    op("v", "copy", (T.lk[:, 18:36], T.gkt[:]), ["gkt"], ["fk1", "fk2"])
+    op("v", "copy", (T.lk[:, 0:18], T.glt[:]), ["glt"], ["fl"])
+
+    def lists():
+        for b in range(4):
+            op("v", "ts", (T.xlo[:, 18 * b:18 * b + 18], T.lk[:, 0:18], 4.0, float(b), A.mult, A.add), ["fl"], ["xlo%d" % b])
+        op("v", "ts", (T.lk2[:], T.lk[:], 2.0, 1.0, A.mult, A.add), ["fl", "fk1", "fk2"], ["lk2"])
+
+    lists()
+    op("v", "quant", (T.qu[:], T.su[:], T.ut[:]), ["ut"], ["qu"])
+    op("v", "copy", (T.qr[:].bitcast(dt.uint32), T.qu[:].bitcast(dt.uint32).indirect(T.ofu[:])), ["qu", "ofu"], ["qr"])
+    op("s", "act", (T.sr[:], T.su[:].indirect(T.ofu[:]), F.Copy), ["qu", "ofu"], ["sr"])
+
+    def lay(h):
+        c, odd, n = slice(H * h, H * h + H), slice(2 * H * h + 1, 2 * H * h + 2 * H, 2), "ab"[h]
+        op("v", "tt", (T.v0[:, odd], T.sg[:, c], T.lab[:, c], A.add), ["sg" + n, "lab", "v0z"], ["V0" + n])
+
+    def half(h, ahead=None):
+        c, e = slice(H * h, H * h + H), slice(4 * H * h, 4 * H * h + 4 * H)
+        n = "ab"[h]
+        op("v", "quant", (T.qx[:, c], T.sx[:, c], T.xt[:, e]), ["X%d" % h], ["qx" + n])
+        op("t", "mm", (T.pb[:, 512 * h:512 * h + H], T.qr[:, 0:128], T.sr[:, 0:128], T.qx[:, c], T.sx[:, c]), ["qr", "sr", "qx" + n], ["pb" + n])
+        if h == 0:
+            op("t", "mm", (T.pt[:, 0:H], T.qr[:, 128:256], T.sr[:, 128:256], T.qx[:, c], T.sx[:, c]), ["qr", "sr", "qx" + n], ["pt"])
+        if ahead is not None:
+            ahead()
+        op("s", "act", (T.sg[:, c], T.pb[:, 512 * h:512 * h + H], F.Sign), ["pb" + n], ["sg" + n], bias=-2.0 ** -100)
+
+    def signs(t, h):
+        n = "ab"[h]
+        op("s", "act", (T["i%d" % t][:, 2 * H * h + 1:2 * H * h + 2 * H:2], T.sg[:, H * h:H * h + H], F.Copy), ["sg" + n], ["i%d%s" % (t, n)], scale=-2.0 * R[t])
+
+    def xl(a, b, key, elements):
+        for t in elements:
+            op("s", "act", (T.zz[:, 64 * a + t:64 * b:4], T.xt[:].indirect(T.xlo[:, 18 * t + a:18 * t + b]), F.Copy), ["X0", "X1", "xlo%d" % t], [key + str(t)])
+
+    def add_x(i, a, b, key):
+        e, keys = slice(64 * a, 64 * b), [key + str(t) for t in range(4)]
+        op("g", "dma", (T.zz[:, e], T.xt[:, e]), ["X0", "X1"] + keys, keys, sem="ga%d" % i, inc=16, accum_op=A.add)
+
+    zk = [k + str(t) for k in ("zA", "zB") for t in range(4)]
+
+    def differences():
+        op("v", "tt", (T.df[:, 0:9], T.lk[:, 27:36], T.lk[:, 0:9], A.subtract), ["fl", "fk2"], ["df0"])
+        op("v", "tt", (T.df[:, 9:18], T.lk[:, 18:27], T.lk[:, 9:18], A.subtract), ["fl", "fk1"], ["df1"])
+
+    def tiles_of_constants():
+        op("g", "iota", (T.et[:], [[0, 2048]], 0, 0), [], ["et"], **imprecise)
+        for b in range(4):
+            op("g", "sel", (T.et[:, 512 * b + b:512 * b + 512:4], T.eye[:], [[-1, 128]], A.is_equal, 0.0, 0, 1), ["eye", "et"], ["et%d" % b])
+        op("g", "iota", (T.c16[:], [[0, 9], [1, 16]], 0, 0), [], ["c16"], **imprecise)
+
+    half(1)
+    signs(1, 1)
+    signs(2, 1)
+    differences()
+    for r in range(3):
+        rs = str(r)
+        half(0, lambda: xl(0, 10, "zA", (0, 1)))
+        lay(1)
+        if r == 0:
+            op("v", "ts", (T.m4[:], T.a4[:], T.pf[:, 2:3], ONE, A.is_equal, A.mult), ["a4", "pf"], ["m4"])
+        lay(0)
+        xl(0, 10, "zA", (2,))
+        for t in range(3):
+            win, wk = T["v%d" % t], (["V0a", "V0b", "v0z"] if t == 0 else ["V%d" % t])
+            own, ok = (T.lab[:], "lab") if t == 0 else (T["g%d" % t][:, 1:2 * C:2], "m%d" % t)
+            op("s", "act", (T.kv[:], win[:].indirect(T.lk2[:, 18:36]), F.Copy), wk + ["lk2"], ["kv"], bias=-R[t])
+            op("v", "tt", (T.yy[:], win[:].indirect(T.lk2[:, 0:18]), own, A.max), wk + ["lk2", ok], ["yy"])
+            if t == 2:
+                break
+            op("v", "tt", (T.dd[:], win[:].indirect(T.lk2[:, 0:18]), T.kv[:], A.subtract), wk + ["lk2", "kv"], ["dd"])
+            if t == 0:
+                signs(1, 0)
+                xl(0, 10, "zA", (3,))
+                add_x(2 * r, 0, 10, "zA")
+            else:
+                xl(10, 18, "zB", (3,))
+                add_x(2 * r + 1, 10, 18, "zB")
+            d1 = T["g%d" % (t + 1)]
+            op("s", "act", (d1[:, 0:2 * C:2], T.dd[:], F.Sign), ["dd"], ["s%d" % (t + 1)], bias=-3.0 * R[t])
+            op("v", "tt", (d1[:, 1:2 * C:2], T.yy[:], T.kv[:], A.max), ["yy", "kv"], ["m%d" % (t + 1)])
+            if t == 0:
+                signs(2, 0)
+                xl(10, 18, "zB", (0, 1, 2))
+            elif r == 0:
+                tiles_of_constants()
+            i1 = "i%d" % (t + 1)
+            op("v", "scan", (T["v%d" % (t + 1)][:], T[i1][:], d1[:], 0.0, A.mult, A.add), [i1 + "a", i1 + "b", i1 + "z", "s%d" % (t + 1), "m%d" % (t + 1)], ["V%d" % (t + 1)])
+        if r == 0:
+            op("v", "ts", (T.rs4[:], T.c4[:], 0, None, A.is_gt), ["c4"], ["rs4"])
+        op("v", "tt", (T.mb[:], T.yy[:], T.kv[:], A.max), ["yy", "kv"], ["mb"])
+        for a in range(4):
+            if a < 2:
+                op("v", "ts", (T.mk[:, a:C:4], T.mb[:, a:C:4], T.m4[:, a:a + 1], None, A.mult), ["mb", "m4"], ["mk%d" % a])
+            else:
+                op("s", "act", (T.mk[:, a:C:4], T.mb[:, a:C:4], F.Copy), ["mb", "m4"], ["mk%d" % a], scale=T.m4[:, a:a + 1])
+        op("v", "scan", (T.sc[:], T.rs4[:], T.mk[:], 0.0, A.mult, A.add), ["rs4", "mk0", "mk1", "mk2", "mk3"], ["sc"])
+        op("v", "copy", (T.oi[:], T.sc[:, 3:C:4]), ["sc"], ["oi"])
+        op("v", "ts", (T.oa[:], T.oi[:], 2047, None, A.bitwise_and), ["oi"], ["oa"])
+        op("v", "copy", (T.oo[:], T.oa[:]), ["oa"], ["oo"])
+        op("v", "ts", (T.zt[:, 0:576], T.zz[:].indirect(T.oo[:, 0:36]), 0.5, None, A.mult), zk + ["oo"], ["zt0"])
+        op("s", "act", (T.zt[:, 576:1152], T.zz[:].indirect(T.oo[:, 36:72]), F.Copy), zk + ["oo"], ["zt1"], scale=0.5)
+        op("v", "quant", (T.qz[:], T.sz[:], T.zt[:]), ["zt0", "zt1"], ["qz"])
+        for b in range(4):
+            op("t", "mm", (T.pr[:, 512 * b:512 * b + C], T.qw[:, 128 * b:128 * b + 128], T.sw[:, 128 * b:128 * b + 128], T.qz[:], T.sz[:]), ["qw", "sw", "qz"], ["pr%d" % b])
+        if r == 0:
+            op("v", "ts", (T.mask4[:], T.c4[:], T.pf[:, 2:3], ONE, A.is_equal, A.mult), ["c4", "pf"], ["mask4"])
+        op("v", "tt", (T.mk2[:], T.mb[:].indirect(T["kin" + rs][:]), T.mask4[:], A.mult), ["mb", "kin" + rs, "mask4"], ["mp"])
+        op("v", "scan", (T.sc2[:], T.rs4[:], T.mk2[:], 0.0, A.mult, A.add), ["rs4", "mp"], ["sc2"])
+        op("v", "copy", (T.mi[:], T.sc2[:, 3:C:4]), ["sc2"], ["mi"])
+        op("v", "ts", (T.ma[:], T.mi[:], 2047, None, A.bitwise_and), ["mi"], ["ma"])
+        op("v", "copy", (T["mm" + rs][:], T.ma[:]), ["ma"], ["mm" + rs])
+        send_m(r)
+        if r > 0:
+            op("v", "tt", (T.mt[:], T.pt[:, 0:H], T.mask16[:], A.mult), ["pt", "mask16"], ["mt"])
+            op("v", "scan", (T.st[:], T.rs16[:], T.mt[:], 0.0, A.mult, A.add), ["rs16", "mt"], ["st"])
+        for b in range(4):
+            src, dst = T.pr[:, 512 * b:512 * b + C], T.ht[:, b:4 * C:4]
+            if b == 3:
+                op("v", "ts", (dst, src, 0.03125, None, A.mult), ["pr%d" % b], ["h%d" % b])
+            else:
+                op("s", "act", (dst, src, F.Copy), ["pr%d" % b], ["h%d" % b], scale=0.03125)
+        hk = ["h0", "h1", "h2", "h3"]
+        op("v", "copy", (T.hs[:, 0:288], T.ht[:].indirect(T["mm" + rs][:, 0:18])), hk + ["mm" + rs], ["hs0"])
+        op("s", "act", (T.hs[:, 288:576], T.ht[:].indirect(T["mm" + rs][:, 18:36]), F.Copy), hk + ["mm" + rs], ["hs1"])
+        op("v", "quant", (T["qh" + rs][:], T["sh" + rs][:], T.hs[:]), ["hs0", "hs1"], ["qh" + rs])
+        send_h(r)
+        if r == 0:
+            op("v", "ts", (T.mask16[:], T.c16[:], T.pf[:, 0:1], None, A.is_equal), ["c16", "pf"], ["mask16"])
+            op("v", "ts", (T.rs16[:], T.c16[:], 0, None, A.is_gt), ["c16"], ["rs16"])
+            op("v", "tt", (T.mt[:], T.pt[:, 0:H], T.mask16[:], A.mult), ["pt", "mask16"], ["mt"])
+            op("v", "scan", (T.st[:], T.rs16[:], T.mt[:], 0.0, A.mult, A.add), ["rs16", "mt"], ["st"])
+        op("v", "ts", (T.tt[:, 0:9], T.st[:, 15:H:16], 0.0, None, A.is_lt), ["st"], ["tt0"])
+        op("v", "ts", (T.tt[:, 9:18], T.st[:, 15:H:16], 0.0, None, A.is_lt), ["st"], ["tt1"])
+        op("v", "tt", (T.dt2[:], T.df[:], T.tt[:], A.mult), ["df0", "df1", "tt0", "tt1"], ["dt2"])
+        op("v", "tt", (T.lk[:, 18:27], T.lk[:, 18:27], T.dt2[:, 9:18], A.subtract), ["fk1", "dt2"], ["fk1"])
+        op("v", "tt", (T.lk[:, 27:36], T.lk[:, 27:36], T.dt2[:, 0:9], A.subtract), ["fk2", "dt2"], ["fk2"])
+        op("v", "tt", (T.lk[:, 0:18], T.lk[:, 0:18], T.dt2[:], A.add), ["fl", "dt2"], ["fl"])
+        if r < 2:
+            op("v", "copy", (T["ks%d" % (r + 1)][:], T.lk[:, 18:36]), ["fk1", "fk2"], ["ks%d" % (r + 1)])
+            send_k(r + 1)
+            lists()
+        else:
+            op("v", "copy", (T.kf[:], T.lk[:]), ["fl", "fk1", "fk2"], ["kf"])
+            op("s", "act", (T.lrow[:], T.lab[:].indirect(T.kf[:]), F.Copy), ["lab", "kf"], ["lrow"], scale=ONE / 4)
+            op("y", "dma", (T.lr[:], T.lrow[0:128:16, :]), ["lrow"], ["lr"], sem="out", inc=16)
+            op("v", "quant", (T.qv[:], T.sv[:], T.vt[:]), ["vt"], ["qv"])
+        if r == 0:
+            op("v", "quant", (T.qe[:], T.se[:], T.et[:]), ["et", "et0", "et1", "et2", "et3"], ["qe"])
+        op("v", "tt", (T.xt[:, 576:1152], T.ht[:].indirect(T["min" + rs][:]), T.xt[:, 576:1152], A.add), hk + ["min" + rs, "X1"], ["X1"])
+        if r < 2:
+            half(1)
+            signs(1, 1)
+            signs(2, 1)
+            differences()
+        else:
+            output(op, T, 1)
+        for b in range(4):
+            op("t", "mm", (T.pr[:, 512 * b:512 * b + H], T.qe[:, 128 * b:128 * b + 128], T.se[:, 128 * b:128 * b + 128], T["qin" + rs][:], T["sin" + rs][:]),
+               ["qe", "qin" + rs], ["pr%d" % b])
+        for b in range(4):
+            op("v", "tt", (T.xt[:, b:576:4], T.xt[:, b:576:4], T.pr[:, 512 * b:512 * b + H], A.add), ["pr%d" % b, "X0e%d" % b], ["X0e%d" % b])
+    output(op, T, 0)
+    for sem, n in sorted(count.items()) + sorted(expect.items()):
+        if waited["g"].get(sem, 0) < n:
+            g.wait_ge(T.sem[sem], n)
+    g.wait_ge(T.sem["sent"], done[0])
+
+
+def output(op, T, h):
+    n, c, e = "ab"[h], slice(H * h, H * h + H), slice(4 * H * h, 4 * H * h + 4 * H)
+    op("v", "quant", (T.qx[:, c], T.sx[:, c], T.xt[:, e]), ["X%d" % h], ["qx" + n])
+    op("t", "mm", (T.pb[:, 512 * h:512 * h + H], T.qv[:], T.sv[:], T.qx[:, c], T.sx[:, c]), ["qv", "qx" + n], ["pb" + n])
+    op("y", "dma", (T.oc[:, e], T.qx[:, c].bitcast(dt.uint8)), ["qx" + n], ["oc" + n], sem="out", inc=16)
+    for k in range(4):
+        op("y", "dma", (T.osc[4 * k:4 * k + 4, c], T.sx[32 * k:32 * k + 4, c]), ["qx" + n], ["osc%s%d" % (n, k)], sem="out", inc=16)
+    op("v", "copy", (T.ys[:, c], T.pb[:, 512 * h:512 * h + H]), ["pb" + n], ["ys" + n])
+    op("s", "dma", (T.y[:, c], T.ys[:, c]), ["ys" + n], ["y" + n], sem="out", inc=16)

@@ -2,9 +2,14 @@ from concourse.bass import DstId, RemoteDMATransfer
 from concourse.mybir import dt, AluOpType as A, ActivationFunctionType as F
 
 N, MASK = 8, [4, 1, 2]
-C, H, G = 288, 144, 4
-R = [0.5, 1.5, 4.5]
-ONE = 4096.0
+C, H = 288, 144
+U = 2.0 ** -118
+TAG = 2048 * U
+OWN, SET = 2, 4
+LIFT = [1, 4, 16]
+CUT = [1, 4]
+STATE = [8, 32]
+BIG = 128 * TAG
 f32, b16, i32, u16, u8, q8 = "float32", "bfloat16", "int32", "uint16", "uint8", "float8_e4m3fn_x4"
 SCRATCH = {
     "xt": ("sbuf", [128, 4 * C], b16), "ut": ("sbuf", [128, 512], b16), "vt": ("sbuf", [128, 512], b16),
@@ -16,28 +21,31 @@ SCRATCH = {
     "qx": ("sbuf", [128, C], q8), "sx": ("sbuf", [128, C], u8),
     "qz": ("sbuf", [128, C], q8), "sz": ("sbuf", [128, C], u8),
     "qe": ("sbuf", [128, 512], q8), "se": ("sbuf", [128, 512], u8),
-    "eye": ("sbuf", [128, 128], b16), "et": ("sbuf", [128, 2048], b16),
-    "pi": ("sbuf", [128, 4], i32), "pa": ("sbuf", [128, 4], i32), "pf": ("sbuf", [128, 4], f32), "a4": ("sbuf", [128, 4], f32), "m4": ("sbuf", [128, 4], f32),
-    "c4": ("sbuf", [128, C], f32), "c16": ("sbuf", [128, H], f32), "labc": ("sbuf", [128, C], f32),
-    "mask4": ("sbuf", [128, C], f32), "mask16": ("sbuf", [128, H], f32), "rs4": ("sbuf", [128, C], f32), "rs16": ("sbuf", [128, H], f32),
-    "lab": ("sbuf", [128, C], f32), "ofi": ("sbuf", [128, 16], i32), "ofu": ("sbuf", [128, 16], u16),
-    "lk": ("sbuf", [128, 36], f32), "df": ("sbuf", [128, 18], f32), "tt": ("sbuf", [128, 18], f32), "dt2": ("sbuf", [128, 18], f32),
-    "lk2": ("sbuf", [128, 36], u16), "kf": ("sbuf", [128, 36], u16),
-    "xlo": ("sbuf", [128, 72], u16), "oo": ("sbuf", [128, 72], u16), "oi": ("sbuf", [128, 72], i32), "oa": ("sbuf", [128, 72], i32),
+    "et": ("sbuf", [128, 516], b16), "cf": ("sbuf", [128, 6 * C + 2], b16),
+    "pi": ("sbuf", [128, 4], i32), "pa": ("sbuf", [128, 4], i32), "pf": ("sbuf", [128, 8], f32),
+    "e16": ("sbuf", [128, 16], f32), "r16": ("sbuf", [128, 16], f32), "r8": ("sbuf", [128, 8], f32), "k8": ("sbuf", [128, 8], f32),
+    "c16": ("sbuf", [128, H], f32), "labc": ("sbuf", [128, C], f32),
+    "mask16": ("sbuf", [128, H], f32), "rs16": ("sbuf", [128, H], f32),
+    "hi": ("sbuf", [128, C], f32), "own": ("sbuf", [128, C], f32), "ofi": ("sbuf", [128, 16], i32), "ofu": ("sbuf", [128, 16], u16),
+    "lk": ("sbuf", [128, 36], f32), "df": ("sbuf", [128, 18], f32), "dt2": ("sbuf", [128, 18], f32),
+    "lf": ("sbuf", [128, 126], f32), "kf": ("sbuf", [128, 36], u16),
+    "oo": ("sbuf", [128, 72], u16), "oi": ("sbuf", [128, 72], i32), "oa": ("sbuf", [128, 72], i32),
     "mi": ("sbuf", [128, 72], i32), "ma": ("sbuf", [128, 72], i32),
     "sg": ("sbuf", [128, C], f32), "v0": ("sbuf", [128, 2 * C], f32), "v1": ("sbuf", [128, 2 * C], f32), "v2": ("sbuf", [128, 2 * C], f32),
-    "i1": ("sbuf", [128, 2 * C], f32), "i2": ("sbuf", [128, 2 * C], f32), "g1": ("sbuf", [128, 2 * C], f32), "g2": ("sbuf", [128, 2 * C], f32),
-    "yy": ("sbuf", [128, C], f32), "kv": ("sbuf", [128, C], f32), "dd": ("sbuf", [128, C], f32), "mb": ("sbuf", [128, C], f32),
-    "mk": ("sbuf", [128, C], f32), "sc": ("sbuf", [128, C], f32), "mk2": ("sbuf", [128, C], f32), "sc2": ("sbuf", [128, C], f32),
+    "g1": ("sbuf", [128, 2 * C], f32), "g2": ("sbuf", [128, 2 * C], f32), "g3": ("sbuf", [128, 2 * C], f32),
+    "kk": ("sbuf", [128, C], f32), "gg": ("sbuf", [128, C], f32), "dd": ("sbuf", [128, C], f32),
+    "sc": ("sbuf", [128, 2 * C], f32), "mp": ("sbuf", [128, 2 * C], f32), "sc2": ("sbuf", [128, 2 * C], f32),
     "mt": ("sbuf", [128, H], f32), "st": ("sbuf", [128, H], f32),
     "lrow": ("sbuf", [128, 2 * C], f32),
     "zz": ("sbuf", [128, 4 * C], b16), "zt": ("sbuf", [128, 4 * C], b16), "ht": ("sbuf", [128, 4 * C], b16), "hs": ("sbuf", [128, 4 * H], b16),
     "ys": ("sbuf", [128, C], f32),
     "pb": ("psum", [128, 1024], f32), "pt": ("psum", [128, 512], f32), "pr": ("psum", [128, 2048], f32),
 }
+HOLD = 4 * C + 1
+XL, L2, K2, KE = 0, 72, 90, 108
 for _r in range(3):
-    SCRATCH["ks%d" % _r] = ("sbuf", [128, 18], u16)
-    SCRATCH["kin%d" % _r] = ("sbuf", [128, 18], u16)
+    SCRATCH["lo%d" % _r] = ("sbuf", [128, 126], u16)
+    SCRATCH["kin%d" % _r] = ("sbuf", [128, 36], u16)
     SCRATCH["mm%d" % _r] = ("sbuf", [128, 72], u16)
     SCRATCH["min%d" % _r] = ("sbuf", [128, 36], u16)
     SCRATCH["qh%d" % _r] = ("sbuf", [128, H], q8)
@@ -47,7 +55,7 @@ for _r in range(3):
 SCRATCH["hq"] = ("sbuf", [128, H // 2], q8)
 SCRATCH["hsc"] = ("sbuf", [128, H // 2], u8)
 SCRATCH["hk"] = ("sbuf", [128, 18], u16)
-SCRATCH["hm"] = ("sbuf", [128, 36], u16)
+SCRATCH["hm"] = ("sbuf", [128, 18], u16)
 SEMAPHORES = ["cv", "cs", "ct", "cg", "sent", "out", "hq", "hs", "hk", "hm"] + ["%s%d" % (n, r) for n in ("ak", "am", "aq") for r in range(3)] \
     + ["ld%d" % i for i in range(8)] + ["ga%d" % i for i in range(6)]
 
@@ -82,9 +90,8 @@ def hand_on(g, core, T, topo):
             n = len(topo.engines(a, core)) // len(hs)
             w, mw = H // len(hs), 36 // len(hs)
             c0 = j * w
-            kw = 18 // len(hs)
             g.wait_ge(T.sem["hk"], n)
-            done += send(g, T, topo, core, b, T["kin%d" % r][:, j * kw:j * kw + kw], T["hk"][:, 0:kw], "ak%d" % r)
+            done += send(g, T, topo, core, b, T["kin%d" % r][:, j * mw:j * mw + mw], T["hk"][:, 0:mw], "ak%d" % r)
             g.wait_ge(T.sem["hm"], n)
             done += send(g, T, topo, core, b, T["min%d" % r][:, j * mw:j * mw + mw], T["hm"][:, 0:mw], "am%d" % r)
             g.wait_ge(T.sem["hq"], n)
@@ -160,8 +167,8 @@ def rank_program(g, core, T, topo):
         expect[sem] = n
         lastw[key] = (sem, n, "far")
 
-    def ship(r, kind, out, in_, width, sem, key):
-        before("g", [key], [])
+    def ship(r, kind, out, in_, width, sem, keys):
+        before("g", keys, [])
         dst = T.cores[rank ^ MASK[r]]
         hs = handers(topo, core, dst)
         if hs is None:
@@ -190,14 +197,14 @@ def rank_program(g, core, T, topo):
         arrives("aq%d" % r, 2 * n, "qin%d" % r)
 
     def send_k(r):
-        ship(r, "hk", lambda c: T["kin%d" % r][:, c], lambda c: T["ks%d" % r][:, c], 18, "ak%d" % r, "ks%d" % r)
+        ship(r, "hk", lambda c: T["kin%d" % r][:, c], lambda c: T["lo%d" % r][:, c.start + K2:c.stop + K2], 36, "ak%d" % r, ["k2_%d" % r, "ke_%d" % r])
 
     def send_m(r):
-        ship(r, "hm", lambda c: T["min%d" % r][:, c], lambda c: T["mm%d" % r][:, c.start + 36:c.stop + 36], 36, "am%d" % r, "mm%d" % r)
+        ship(r, "hm", lambda c: T["min%d" % r][:, c], lambda c: T["mm%d" % r][:, c.start + 36:c.stop + 36], 36, "am%d" % r, ["mm%d" % r])
 
     def send_h(r):
-        ship(r, "hq", lambda c: T["qin%d" % r][:, c].bitcast(dt.uint8), lambda c: T["qh%d" % r][:, c].bitcast(dt.uint8), H, "aq%d" % r, "qh%d" % r)
-        ship(r, "hs", lambda c: T["sin%d" % r][:, c], lambda c: T["sh%d" % r][:, c], H, "aq%d" % r, "qh%d" % r)
+        ship(r, "hq", lambda c: T["qin%d" % r][:, c].bitcast(dt.uint8), lambda c: T["qh%d" % r][:, c].bitcast(dt.uint8), H, "aq%d" % r, ["qh%d" % r])
+        ship(r, "hs", lambda c: T["sin%d" % r][:, c], lambda c: T["sh%d" % r][:, c], H, "aq%d" % r, ["qh%d" % r])
 
     imprecise = {"allow_small_or_imprecise_dtypes": True}
     load("y", 0, T.gkt[:], T.gk[:], "gkt")
@@ -207,59 +214,82 @@ def rank_program(g, core, T, topo):
     load("y", 4, T.xt[:, 0:576], T.x[:, 0:576], "X0")
     load("y", 5, T.qw[:].bitcast(dt.uint8), T.wc[:], "qw")
     load("y", 6, T.sw[:], T.ws[:], "sw")
-    load("y", 7, T.vt[:], T.v[:], "vt")
     op("g", "iota", (T.pi[:], [[0, 4]], 0, 1), [], ["pi"])
-    op("g", "iota", (T.a4[:], [[1, 4]], 0, 0), [], ["a4"], **imprecise)
-    op("g", "iota", (T.ofi[:], [[1, 2], [16, 8]], 0, 0), [], ["ofi"])
+    op("g", "iota", (T.e16[:], [[0, 2], [1, 8]], 0, 0), [], ["e16"], **imprecise)
     op("g", "iota", (T.labc[:], [[4, C]], 0, 0), [], ["labc"], **imprecise)
-    op("g", "iota", (T.c4[:], [[0, 72], [1, 4]], 0, 0), [], ["c4"], **imprecise)
-    op("v", "memset", (T.eye[:], 1.0), [], ["eye"])
-    op("v", "memset", (T.v0[:, 0:2 * C:2], 0.0), [], ["v0z"])
-    op("v", "memset", (T.i1[:, 0:2 * C:2], 0.0), [], ["i1z"])
-    op("v", "memset", (T.i2[:, 0:2 * C:2], 0.0), [], ["i2z"])
-    op("v", "ts", (T.pa[:, 0:1], T.pi[:, 0:1], 15, None, A.bitwise_and), ["pi"], ["pa0"])
+    op("g", "iota", (T.ofi[:], [[1, 2], [16, 8]], 0, 0), [], ["ofi"])
+    op("g", "iota", (T.v0[:, 0:2 * C:2], [[0, C]], 0, 0), [], ["v0z"], **imprecise)
+    op("v", "memset", (T.et[:], 1.0), [], ["et"])
+    op("g", "sel", (T.et[:], T.et[:], [[-1, 516]], A.is_equal, 0.0, 3, 4), ["et"], ["et"])
+    op("g", "dma", (T.vt[:], T.v[:]), [], ["vt"], sem="ld7", inc=16)
     op("v", "ts", (T.pa[:, 1:2], T.pi[:, 1:2], 3, None, A.bitwise_and), ["pi"], ["pa1"])
-    op("v", "copy", (T.ofu[:], T.ofi[:]), ["ofi"], ["ofu"])
-    op("v", "ts", (T.pa[:, 2:3], T.pa[:, 0:1], 2, None, A.logical_shift_right), ["pa0"], ["pa2"])
+    op("v", "ts", (T.pa[:, 2:3], T.pi[:, 2:3], 12, 1, A.bitwise_and, A.logical_shift_right), ["pi"], ["pa2"])
+    op("v", "ts", (T.pa[:, 0:1], T.pi[:, 0:1], 15, None, A.bitwise_and), ["pi"], ["pa0"])
     op("v", "copy", (T.pf[:, 0:3], T.pa[:, 0:3]), ["pa0", "pa1", "pa2"], ["pf"])
-    op("v", "ts", (T.lab[:], T.labc[:], T.pf[:, 1:2], 1.0 / ONE, A.add, A.mult), ["labc", "pf"], ["lab"])
-    op("v", "copy", (T.ks0[:], T.gkt[:]), ["gkt"], ["ks0"])
+    op("v", "memset", (T.cf[:, 0:HOLD + 2 * C:2], 0.0), [], ["cfz"])
+    op("v", "ts", (T.pf[:, 4:5], T.pf[:, 1:2], U, SET * TAG, A.mult, A.add), ["pf"], ["pf4"])
+    op("v", "ts", (T.r16[:], T.e16[:], T.pf[:, 2:3], BIG, A.is_equal, A.mult), ["e16", "pf"], ["r16"])
+    op("v", "copy", (T.ofu[:], T.ofi[:]), ["ofi"], ["ofu"])
+    op("v", "ts", (T.r8[:], T.r16[:, 8:16], -2.0, None, A.mult), ["r16"], ["r8"])
+    op("v", "tt", (T.k8[:], T.r8[:], T.r16[:, 6:14], A.add), ["r8", "r16"], ["k8"])
+    op("s", "act", (T.hi[:], T.labc[:], F.Identity), ["labc", "pf4"], ["hi"], scale=U, bias=T.pf[:, 4:5])
+    op("s", "act", (T.own[:], T.hi[:], F.Copy), ["hi"], ["own"], bias=(OWN - SET) * TAG)
+    for e in range(0, 8, 2):
+        op("s", "act", (T.cf[:, HOLD + e:HOLD + 2 * C:8], T.labc[:, 0:72], F.Identity), ["labc", "k8"], ["hold%d" % e], scale=0.0, bias=T.k8[:, e:e + 1])
+    hold, held = T.cf[:, HOLD:HOLD + 2 * C], ["cfz"] + ["hold%d" % e for e in range(0, 8, 2)]
+
+    def lkeys(r):
+        return ["xl%d_%d" % (t, r) for t in range(4)] + ["l2_%d" % r, "k2_%d" % r, "ke_%d" % r]
+
+    def lists(r):
+        for t in range(4):
+            op("s", "act", (T.lf[:, 18 * t:18 * t + 18], T.lk[:, 0:18], F.Copy), ["fl"], ["lf%d" % t], scale=4.0, bias=float(t))
+        op("s", "act", (T.lf[:, L2:L2 + 18], T.lk[:, 0:18], F.Copy), ["fl"], ["lf4"], scale=2.0, bias=1.0)
+        for i, (at, add) in enumerate(((K2, 1.0), (KE, 0.0))):
+            op("s", "act", (T.lf[:, at:at + 9], T.lk[:, 27:36], F.Copy), ["fk"], ["lf%d" % (5 + 2 * i)], scale=2.0, bias=add)
+            op("s", "act", (T.lf[:, at + 9:at + 18], T.lk[:, 18:27], F.Copy), ["fk"], ["lf%d" % (6 + 2 * i)], scale=2.0, bias=add)
+
+    def convert(r):
+        op("v", "copy", (T["lo%d" % r][:], T.lf[:]), ["lf%d" % i for i in range(9)], lkeys(r))
+
+    op("v", "ts", (T.lo0[:, K2:K2 + 18], T.gkt[:], 2.0, 1.0, A.mult, A.add), ["gkt"], ["k2_0"])
+    op("v", "ts", (T.lo0[:, KE:KE + 18], T.gkt[:], 2.0, None, A.mult), ["gkt"], ["ke_0"])
     send_k(0)
-    op("v", "copy", (T.lk[:, 18:36], T.gkt[:]), ["gkt"], ["fk1", "fk2"])
-    op("v", "copy", (T.lk[:, 0:18], T.glt[:]), ["glt"], ["fl"])
-
-    def lists():
-        for b in range(4):
-            op("v", "ts", (T.xlo[:, 18 * b:18 * b + 18], T.lk[:, 0:18], 4.0, float(b), A.mult, A.add), ["fl"], ["xlo%d" % b])
-        op("v", "ts", (T.lk2[:], T.lk[:], 2.0, 1.0, A.mult, A.add), ["fl", "fk1", "fk2"], ["lk2"])
-
-    lists()
+    op("g", "iota", (T.c16[:], [[0, 9], [1, 16]], 0, 0), [], ["c16"], **imprecise)
+    op("v", "ts", (T.lo0[:, L2:L2 + 18], T.glt[:], 2.0, 1.0, A.mult, A.add), ["glt"], ["l2_0"])
+    for t in range(4):
+        op("v", "ts", (T.lo0[:, 18 * t:18 * t + 18], T.glt[:], 4.0, float(t), A.mult, A.add), ["glt"], ["xl%d_0" % t])
     op("v", "quant", (T.qu[:], T.su[:], T.ut[:]), ["ut"], ["qu"])
     op("v", "copy", (T.qr[:].bitcast(dt.uint32), T.qu[:].bitcast(dt.uint32).indirect(T.ofu[:])), ["qu", "ofu"], ["qr"])
     op("s", "act", (T.sr[:], T.su[:].indirect(T.ofu[:]), F.Copy), ["qu", "ofu"], ["sr"])
 
-    def lay(h):
-        c, odd, n = slice(H * h, H * h + H), slice(2 * H * h + 1, 2 * H * h + 2 * H, 2), "ab"[h]
-        op("v", "tt", (T.v0[:, odd], T.sg[:, c], T.lab[:, c], A.add), ["sg" + n, "lab", "v0z"], ["V0" + n])
-
-    def half(h, ahead=None):
+    def scores(h):
         c, e = slice(H * h, H * h + H), slice(4 * H * h, 4 * H * h + 4 * H)
         n = "ab"[h]
         op("v", "quant", (T.qx[:, c], T.sx[:, c], T.xt[:, e]), ["X%d" % h], ["qx" + n])
         op("t", "mm", (T.pb[:, 512 * h:512 * h + H], T.qr[:, 0:128], T.sr[:, 0:128], T.qx[:, c], T.sx[:, c]), ["qr", "sr", "qx" + n], ["pb" + n])
         if h == 0:
             op("t", "mm", (T.pt[:, 0:H], T.qr[:, 128:256], T.sr[:, 128:256], T.qx[:, c], T.sx[:, c]), ["qr", "sr", "qx" + n], ["pt"])
-        if ahead is not None:
-            ahead()
-        op("s", "act", (T.sg[:, c], T.pb[:, 512 * h:512 * h + H], F.Sign), ["pb" + n], ["sg" + n], bias=-2.0 ** -100)
 
-    def signs(t, h):
+    def lay(h):
+        c, odd, n = slice(H * h, H * h + H), slice(2 * H * h + 1, 2 * H * h + 2 * H, 2), "ab"[h]
+        op("v", "tt", (T.v0[:, odd], T.pb[:, 512 * h:512 * h + H], T.hi[:, c], A.min), ["pb" + n, "hi", "v0z"], ["V0" + n])
+
+    def sign(h):
         n = "ab"[h]
-        op("s", "act", (T["i%d" % t][:, 2 * H * h + 1:2 * H * h + 2 * H:2], T.sg[:, H * h:H * h + H], F.Copy), ["sg" + n], ["i%d%s" % (t, n)], scale=-2.0 * R[t])
+        op("s", "act", (T.sg[:, H * h:H * h + H], T.v0[:, 2 * H * h + 1:2 * H * h + 2 * H:2], F.Sign), ["V0" + n], ["sg" + n], bias=-TAG)
 
-    def xl(a, b, key, elements):
-        for t in elements:
-            op("s", "act", (T.zz[:, 64 * a + t:64 * b:4], T.xt[:].indirect(T.xlo[:, 18 * t + a:18 * t + b]), F.Copy), ["X0", "X1", "xlo%d" % t], [key + str(t)])
+    def factor(t, h, q="s"):
+        n, at, by = "ab"[h], 2 * C * (t - 1) + 2 * H * h, -STATE[t - 1] * TAG
+        out, in_ = T.cf[:, at + 1:at + 2 * H:2], T.sg[:, H * h:H * h + H]
+        if q == "s":
+            op("s", "act", (out, in_, F.Copy), ["sg" + n], ["i%d%s" % (t, n)], scale=by)
+        else:
+            op("v", "ts", (out, in_, by, None, A.mult), ["sg" + n], ["i%d%s" % (t, n)])
+
+    def xl(r, t, a, b):
+        op("s", "act", (T.zz[:, 64 * a + t:64 * b:4], T.xt[:].indirect(T["lo%d" % r][:, 18 * t + a:18 * t + b]), F.Copy), ["X0", "X1", "xl%d_%d" % (t, r)],
+           [k + str(t) for k, (c, d) in (("zA", (0, 10)), ("zB", (10, 18))) if a <= c and d <= b])
 
     def add_x(i, a, b, key):
         e, keys = slice(64 * a, 64 * b), [key + str(t) for t in range(4)]
@@ -267,81 +297,77 @@ def rank_program(g, core, T, topo):
 
     zk = [k + str(t) for k in ("zA", "zB") for t in range(4)]
 
-    def differences():
-        op("v", "tt", (T.df[:, 0:9], T.lk[:, 27:36], T.lk[:, 0:9], A.subtract), ["fl", "fk2"], ["df0"])
-        op("v", "tt", (T.df[:, 9:18], T.lk[:, 18:27], T.lk[:, 9:18], A.subtract), ["fl", "fk1"], ["df1"])
+    def unpacker(b):
+        c = slice(128 * b, 128 * b + 128)
+        op("v", "quant", (T.qe[:, c], T.se[:, c], T.et[:, 3 - b:515 - b]), ["et"], ["qe%d" % b])
 
-    def tiles_of_constants():
-        op("g", "iota", (T.et[:], [[0, 2048]], 0, 0), [], ["et"], **imprecise)
-        for b in range(4):
-            op("g", "sel", (T.et[:, 512 * b + b:512 * b + 512:4], T.eye[:], [[-1, 128]], A.is_equal, 0.0, 0, 1), ["eye", "et"], ["et%d" % b])
-        op("g", "iota", (T.c16[:], [[0, 9], [1, 16]], 0, 0), [], ["c16"], **imprecise)
+    def offsets(row, key, whole, low, out, okey):
+        op("v", "ts", (T[whole][:], row[:, 7:2 * C:8], 2.0 ** 59, 2.0 ** 59, A.mult, A.mult), [key], [whole])
+        op("v", "ts", (T[low][:], T[whole][:], 2047, None, A.bitwise_and), [whole], [low])
+        op("v", "copy", (out[:], T[low][:]), [low], [okey])
 
-    half(1)
-    signs(1, 1)
-    signs(2, 1)
-    differences()
+    scores(1)
     for r in range(3):
         rs = str(r)
-        half(0, lambda: xl(0, 10, "zA", (0, 1)))
-        lay(1)
+        lo = T["lo" + rs]
+        byl, byk = lo[:, L2:L2 + 18], lo[:, K2:K2 + 18]
+        scores(0)
         if r == 0:
-            op("v", "ts", (T.m4[:], T.a4[:], T.pf[:, 2:3], ONE, A.is_equal, A.mult), ["a4", "pf"], ["m4"])
+            lay(1)
+            xl(r, 0, 0, 18)
+            sign(1)
+            factor(1, 1)
+        else:
+            op("v", "tt", (T.df[:], T.lk[:, 18:36], T.lk[:, 0:18], A.subtract), ["fl", "fk"], ["df"])
+            xl(r, 0, 0, 18)
         lay(0)
-        xl(0, 10, "zA", (2,))
+        xl(r, 1, 0, 18)
         for t in range(3):
             win, wk = T["v%d" % t], (["V0a", "V0b", "v0z"] if t == 0 else ["V%d" % t])
-            own, ok = (T.lab[:], "lab") if t == 0 else (T["g%d" % t][:, 1:2 * C:2], "m%d" % t)
-            op("s", "act", (T.kv[:], win[:].indirect(T.lk2[:, 18:36]), F.Copy), wk + ["lk2"], ["kv"], bias=-R[t])
-            op("v", "tt", (T.yy[:], win[:].indirect(T.lk2[:, 0:18]), own, A.max), wk + ["lk2", ok], ["yy"])
+            own, ok = (T.own[:], "own") if t == 0 else (T["g%d" % t][:, 1:2 * C:2], "m%d" % t)
+            kk, gg = (T.g3[:, 0:2 * C:2], T.g3[:, 1:2 * C:2]) if t == 2 else (T.kk[:], T.gg[:])
+            kn, gn = ("kk3", "gg3") if t == 2 else ("kk", "gg")
+            op("v", "tt", (kk, win[:].indirect(byk), own, A.max), wk + ["k2_" + rs, ok], [kn])
+            op("s", "act", (gg, win[:].indirect(byl), F.Copy), wk + ["l2_" + rs], [gn], bias=LIFT[t] * TAG)
             if t == 2:
+                if r == 0:
+                    unpacker(0)
                 break
-            op("v", "tt", (T.dd[:], win[:].indirect(T.lk2[:, 0:18]), T.kv[:], A.subtract), wk + ["lk2", "kv"], ["dd"])
+            op("v", "tt", (T.dd[:], win[:].indirect(byl), T.kk[:], A.subtract), wk + ["l2_" + rs, "kk"], ["dd"])
             if t == 0:
-                signs(1, 0)
-                xl(0, 10, "zA", (3,))
-                add_x(2 * r, 0, 10, "zA")
+                sign(0)
             else:
-                xl(10, 18, "zB", (3,))
-                add_x(2 * r + 1, 10, 18, "zB")
+                factor(2, 0)
+                if r == 0:
+                    factor(2, 1)
             d1 = T["g%d" % (t + 1)]
-            op("s", "act", (d1[:, 0:2 * C:2], T.dd[:], F.Sign), ["dd"], ["s%d" % (t + 1)], bias=-3.0 * R[t])
-            op("v", "tt", (d1[:, 1:2 * C:2], T.yy[:], T.kv[:], A.max), ["yy", "kv"], ["m%d" % (t + 1)])
+            op("s", "act", (d1[:, 0:2 * C:2], T.dd[:], F.Sign), ["dd"], ["s%d" % (t + 1)], bias=-CUT[t] * TAG)
+            op("v", "tt", (d1[:, 1:2 * C:2], T.kk[:], T.gg[:], A.max), ["kk", "gg"], ["m%d" % (t + 1)])
             if t == 0:
-                signs(2, 0)
-                xl(10, 18, "zB", (0, 1, 2))
-            elif r == 0:
-                tiles_of_constants()
+                factor(1, 0)
+                for i, (a, b, key) in enumerate(((0, 10, "zA"), (10, 18, "zB"))):
+                    xl(r, 2, a, b)
+                    xl(r, 3, a, b)
+                    add_x(2 * r + i, a, b, key)
             i1 = "i%d" % (t + 1)
-            op("v", "scan", (T["v%d" % (t + 1)][:], T[i1][:], d1[:], 0.0, A.mult, A.add), [i1 + "a", i1 + "b", i1 + "z", "s%d" % (t + 1), "m%d" % (t + 1)], ["V%d" % (t + 1)])
-        if r == 0:
-            op("v", "ts", (T.rs4[:], T.c4[:], 0, None, A.is_gt), ["c4"], ["rs4"])
-        op("v", "tt", (T.mb[:], T.yy[:], T.kv[:], A.max), ["yy", "kv"], ["mb"])
-        for a in range(4):
-            if a < 2:
-                op("v", "ts", (T.mk[:, a:C:4], T.mb[:, a:C:4], T.m4[:, a:a + 1], None, A.mult), ["mb", "m4"], ["mk%d" % a])
-            else:
-                op("s", "act", (T.mk[:, a:C:4], T.mb[:, a:C:4], F.Copy), ["mb", "m4"], ["mk%d" % a], scale=T.m4[:, a:a + 1])
-        op("v", "scan", (T.sc[:], T.rs4[:], T.mk[:], 0.0, A.mult, A.add), ["rs4", "mk0", "mk1", "mk2", "mk3"], ["sc"])
-        op("v", "copy", (T.oi[:], T.sc[:, 3:C:4]), ["sc"], ["oi"])
-        op("v", "ts", (T.oa[:], T.oi[:], 2047, None, A.bitwise_and), ["oi"], ["oa"])
-        op("v", "copy", (T.oo[:], T.oa[:]), ["oa"], ["oo"])
+            op("v", "scan", (T["v%d" % (t + 1)][:], T.cf[:, 2 * C * t:2 * C * t + 2 * C], d1[:], 0.0, A.mult, A.add),
+               [i1 + "a", i1 + "b", "cfz", "s%d" % (t + 1), "m%d" % (t + 1)], ["V%d" % (t + 1)])
+        op("v", "scan", (T.sc[:], hold, T.g3[:], 0.0, A.add, A.max), held + ["kk3", "gg3"], ["sc"])
+        op("s", "act", (T.mp[:, 1:2 * C:2], T.g3[:].indirect(T["kin" + rs][:, 0:18]), F.Copy), ["kk3", "gg3", "kin" + rs], ["mp1"])
+        op("s", "act", (T.mp[:, 0:2 * C:2], T.g3[:].indirect(T["kin" + rs][:, 18:36]), F.Copy), ["kk3", "gg3", "kin" + rs], ["mp0"])
+        offsets(T.sc, "sc", "oi", "oa", T.oo, "oo")
         op("v", "ts", (T.zt[:, 0:576], T.zz[:].indirect(T.oo[:, 0:36]), 0.5, None, A.mult), zk + ["oo"], ["zt0"])
         op("s", "act", (T.zt[:, 576:1152], T.zz[:].indirect(T.oo[:, 36:72]), F.Copy), zk + ["oo"], ["zt1"], scale=0.5)
+        if r == 0:
+            op("s", "act", (T.rs16[:], T.c16[:], F.Sign), ["c16"], ["rs16"])
+            op("s", "act", (T.mt[:], T.c16[:], F.Abs), ["c16", "pf"], ["mt"], scale=-1.0, bias=T.pf[:, 0:1])
+            op("s", "act", (T.mask16[:], T.mt[:], F.Copy), ["mt"], ["mask16"], scale=-1e28)
         op("v", "quant", (T.qz[:], T.sz[:], T.zt[:]), ["zt0", "zt1"], ["qz"])
         for b in range(4):
             op("t", "mm", (T.pr[:, 512 * b:512 * b + C], T.qw[:, 128 * b:128 * b + 128], T.sw[:, 128 * b:128 * b + 128], T.qz[:], T.sz[:]), ["qw", "sw", "qz"], ["pr%d" % b])
-        if r == 0:
-            op("v", "ts", (T.mask4[:], T.c4[:], T.pf[:, 2:3], ONE, A.is_equal, A.mult), ["c4", "pf"], ["mask4"])
-        op("v", "tt", (T.mk2[:], T.mb[:].indirect(T["kin" + rs][:]), T.mask4[:], A.mult), ["mb", "kin" + rs, "mask4"], ["mp"])
-        op("v", "scan", (T.sc2[:], T.rs4[:], T.mk2[:], 0.0, A.mult, A.add), ["rs4", "mp"], ["sc2"])
-        op("v", "copy", (T.mi[:], T.sc2[:, 3:C:4]), ["sc2"], ["mi"])
-        op("v", "ts", (T.ma[:], T.mi[:], 2047, None, A.bitwise_and), ["mi"], ["ma"])
-        op("v", "copy", (T["mm" + rs][:], T.ma[:]), ["ma"], ["mm" + rs])
+        op("v", "scan", (T.sc2[:], hold, T.mp[:], 0.0, A.add, A.max), held + ["mp0", "mp1"], ["sc2"])
+        offsets(T.sc2, "sc2", "mi", "ma", T["mm" + rs], "mm" + rs)
         send_m(r)
-        if r > 0:
-            op("v", "tt", (T.mt[:], T.pt[:, 0:H], T.mask16[:], A.mult), ["pt", "mask16"], ["mt"])
-            op("v", "scan", (T.st[:], T.rs16[:], T.mt[:], 0.0, A.mult, A.add), ["rs16", "mt"], ["st"])
         for b in range(4):
             src, dst = T.pr[:, 512 * b:512 * b + C], T.ht[:, b:4 * C:4]
             if b == 3:
@@ -351,41 +377,48 @@ def rank_program(g, core, T, topo):
         hk = ["h0", "h1", "h2", "h3"]
         op("v", "copy", (T.hs[:, 0:288], T.ht[:].indirect(T["mm" + rs][:, 0:18])), hk + ["mm" + rs], ["hs0"])
         op("s", "act", (T.hs[:, 288:576], T.ht[:].indirect(T["mm" + rs][:, 18:36]), F.Copy), hk + ["mm" + rs], ["hs1"])
+        if r == 0:
+            unpacker(1)
         op("v", "quant", (T["qh" + rs][:], T["sh" + rs][:], T.hs[:]), ["hs0", "hs1"], ["qh" + rs])
         send_h(r)
         if r == 0:
-            op("v", "ts", (T.mask16[:], T.c16[:], T.pf[:, 0:1], None, A.is_equal), ["c16", "pf"], ["mask16"])
-            op("v", "ts", (T.rs16[:], T.c16[:], 0, None, A.is_gt), ["c16"], ["rs16"])
-            op("v", "tt", (T.mt[:], T.pt[:, 0:H], T.mask16[:], A.mult), ["pt", "mask16"], ["mt"])
-            op("v", "scan", (T.st[:], T.rs16[:], T.mt[:], 0.0, A.mult, A.add), ["rs16", "mt"], ["st"])
-        op("v", "ts", (T.tt[:, 0:9], T.st[:, 15:H:16], 0.0, None, A.is_lt), ["st"], ["tt0"])
-        op("v", "ts", (T.tt[:, 9:18], T.st[:, 15:H:16], 0.0, None, A.is_lt), ["st"], ["tt1"])
-        op("v", "tt", (T.dt2[:], T.df[:], T.tt[:], A.mult), ["df0", "df1", "tt0", "tt1"], ["dt2"])
-        op("v", "tt", (T.lk[:, 18:27], T.lk[:, 18:27], T.dt2[:, 9:18], A.subtract), ["fk1", "dt2"], ["fk1"])
-        op("v", "tt", (T.lk[:, 27:36], T.lk[:, 27:36], T.dt2[:, 0:9], A.subtract), ["fk2", "dt2"], ["fk2"])
-        op("v", "tt", (T.lk[:, 0:18], T.lk[:, 0:18], T.dt2[:], A.add), ["fl", "dt2"], ["fl"])
-        if r < 2:
-            op("v", "copy", (T["ks%d" % (r + 1)][:], T.lk[:, 18:36]), ["fk1", "fk2"], ["ks%d" % (r + 1)])
-            send_k(r + 1)
-            lists()
+            unpacker(2)
+            unpacker(3)
+            op("v", "tt", (T.df[:, 0:9], T.gkt[:, 9:18], T.glt[:, 0:9], A.subtract), ["glt", "gkt"], ["df"])
+            op("v", "tt", (T.df[:, 9:18], T.gkt[:, 0:9], T.glt[:, 9:18], A.subtract), ["glt", "gkt"], ["df1"])
+        op("v", "tt", (T.mt[:], T.pt[:, 0:H], T.mask16[:], A.is_lt), ["pt", "mask16"], ["mt"])
+        op("v", "scan", (T.st[:], T.rs16[:], T.mt[:], 0.0, A.mult, A.add), ["rs16", "mt"], ["st"])
+        op("v", "tt", (T.dt2[:, 0:9], T.df[:, 0:9], T.st[:, 15:H:16], A.mult), ["df", "st"], ["dt0"])
+        op("v", "tt", (T.dt2[:, 9:18], T.df[:, 9:18], T.st[:, 15:H:16], A.mult), ["df", "df1", "st"], ["dt1"])
+        if r == 0:
+            op("v", "tt", (T.lk[:, 18:27], T.gkt[:, 9:18], T.dt2[:, 0:9], A.subtract), ["gkt", "dt0"], ["fk0"])
+            op("v", "tt", (T.lk[:, 27:36], T.gkt[:, 0:9], T.dt2[:, 9:18], A.subtract), ["gkt", "dt1", "fk0"], ["fk"])
         else:
-            op("v", "copy", (T.kf[:], T.lk[:]), ["fl", "fk1", "fk2"], ["kf"])
-            op("s", "act", (T.lrow[:], T.lab[:].indirect(T.kf[:]), F.Copy), ["lab", "kf"], ["lrow"], scale=ONE / 4)
+            op("v", "tt", (T.lk[:, 18:36], T.lk[:, 18:36], T.dt2[:], A.subtract), ["fk", "dt0", "dt1"], ["fk"])
+        op("v", "tt", (T.lk[:, 0:18], (T.lk[:, 0:18] if r else T.glt[:]), T.dt2[:], A.add), ["fl", "glt", "dt0", "dt1"], ["fl"])
+        if r < 2:
+            lists(r + 1)
+        else:
+            op("v", "copy", (T.kf[:, 0:18], T.lk[:, 0:18]), ["fl"], ["kf0"])
+            op("v", "copy", (T.kf[:, 18:27], T.lk[:, 27:36]), ["fk"], ["kf1"])
+            op("v", "copy", (T.kf[:, 27:36], T.lk[:, 18:27]), ["fk"], ["kf2"])
+            op("s", "act", (T.lrow[:], T.labc[:].indirect(T.kf[:]), F.Copy), ["labc", "kf0", "kf1", "kf2"], ["lrow"], scale=0.25)
             op("y", "dma", (T.lr[:], T.lrow[0:128:16, :]), ["lrow"], ["lr"], sem="out", inc=16)
             op("v", "quant", (T.qv[:], T.sv[:], T.vt[:]), ["vt"], ["qv"])
-        if r == 0:
-            op("v", "quant", (T.qe[:], T.se[:], T.et[:]), ["et", "et0", "et1", "et2", "et3"], ["qe"])
         op("v", "tt", (T.xt[:, 576:1152], T.ht[:].indirect(T["min" + rs][:]), T.xt[:, 576:1152], A.add), hk + ["min" + rs, "X1"], ["X1"])
         if r < 2:
-            half(1)
-            signs(1, 1)
-            signs(2, 1)
-            differences()
+            scores(1)
+            convert(r + 1)
+            send_k(r + 1)
+            lay(1)
+            sign(1)
+            factor(1, 1)
+            factor(2, 1)
         else:
             output(op, T, 1)
         for b in range(4):
             op("t", "mm", (T.pr[:, 512 * b:512 * b + H], T.qe[:, 128 * b:128 * b + 128], T.se[:, 128 * b:128 * b + 128], T["qin" + rs][:], T["sin" + rs][:]),
-               ["qe", "qin" + rs], ["pr%d" % b])
+               ["qe%d" % b, "qin" + rs], ["pr%d" % b])
         for b in range(4):
             op("v", "tt", (T.xt[:, b:576:4], T.xt[:, b:576:4], T.pr[:, 512 * b:512 * b + H], A.add), ["pr%d" % b, "X0e%d" % b], ["X0e%d" % b])
     output(op, T, 0)

@@ -4,12 +4,13 @@ from concourse.mybir import dt, AluOpType as A, ActivationFunctionType as F
 N, MASK = 8, [4, 1, 2]
 C, H = 288, 144
 U = 2.0 ** -118
-TAG = 2048 * U
-OWN, SET = 2, 4
-LIFT = [1, 4, 16]
-CUT = [1, 4]
-STATE = [8, 32]
-BIG = 128 * TAG
+T1 = 2048.0
+TAG = T1 * U
+OWN, SET, CUT, STATE = 2, 4, 1, 40
+SINK, SHIFT = 24, 24
+LIFT = [1, 4, 24]
+BIG = 128 * T1
+HV = 20
 f32, b16, i32, u16, u8, q8 = "float32", "bfloat16", "int32", "uint16", "uint8", "float8_e4m3fn_x4"
 SCRATCH = {
     "xt": ("sbuf", [128, 4 * C], b16), "ut": ("sbuf", [128, 512], b16), "vt": ("sbuf", [128, 512], b16),
@@ -21,30 +22,29 @@ SCRATCH = {
     "qx": ("sbuf", [128, C], q8), "sx": ("sbuf", [128, C], u8),
     "qz": ("sbuf", [128, C], q8), "sz": ("sbuf", [128, C], u8),
     "qe": ("sbuf", [128, 512], q8), "se": ("sbuf", [128, 512], u8),
-    "et": ("sbuf", [128, 516], b16), "cf": ("sbuf", [128, 6 * C + 2], b16),
-    "pi": ("sbuf", [128, 4], i32), "pa": ("sbuf", [128, 4], i32), "pf": ("sbuf", [128, 8], f32),
+    "et": ("sbuf", [128, 516], b16), "ea": ("sbuf", [128, 128], f32), "cf": ("sbuf", [128, 4 * C + 2], b16),
+    "pi": ("sbuf", [128, 4], i32), "pa": ("sbuf", [128, 4], i32), "pf": ("sbuf", [128, 8], f32), "up": ("sbuf", [128, 4], f32),
     "e16": ("sbuf", [128, 16], f32), "r16": ("sbuf", [128, 16], f32), "r8": ("sbuf", [128, 8], f32), "k8": ("sbuf", [128, 8], f32),
     "c16": ("sbuf", [128, H], f32), "labc": ("sbuf", [128, C], f32),
     "mask16": ("sbuf", [128, H], f32), "rs16": ("sbuf", [128, H], f32),
     "hi": ("sbuf", [128, C], f32), "own": ("sbuf", [128, C], f32), "ofi": ("sbuf", [128, 16], i32), "ofu": ("sbuf", [128, 16], u16),
     "lk": ("sbuf", [128, 36], f32), "df": ("sbuf", [128, 18], f32), "dt2": ("sbuf", [128, 18], f32),
-    "lf": ("sbuf", [128, 126], f32), "kf": ("sbuf", [128, 36], u16),
-    "oo": ("sbuf", [128, 72], u16), "oi": ("sbuf", [128, 72], i32), "oa": ("sbuf", [128, 72], i32),
-    "mi": ("sbuf", [128, 72], i32), "ma": ("sbuf", [128, 72], i32),
-    "sg": ("sbuf", [128, C], f32), "v0": ("sbuf", [128, 2 * C], f32), "v1": ("sbuf", [128, 2 * C], f32), "v2": ("sbuf", [128, 2 * C], f32),
-    "g1": ("sbuf", [128, 2 * C], f32), "g2": ("sbuf", [128, 2 * C], f32), "g3": ("sbuf", [128, 2 * C], f32),
-    "kk": ("sbuf", [128, C], f32), "gg": ("sbuf", [128, C], f32), "dd": ("sbuf", [128, C], f32),
-    "sc": ("sbuf", [128, 2 * C], f32), "mp": ("sbuf", [128, 2 * C], f32), "sc2": ("sbuf", [128, 2 * C], f32),
+    "lf": ("sbuf", [128, 162], f32), "kf": ("sbuf", [128, 36], u16),
+    "oo": ("sbuf", [128, 72], u16), "oa": ("sbuf", [128, 72], i32), "ma": ("sbuf", [128, 72], i32),
+    "sg": ("sbuf", [128, C], f32), "v0": ("sbuf", [128, 2 * C], f32), "v1": ("sbuf", [128, 2 * C], f32), "v2": ("sbuf", [128, 3 * C], f32),
+    "g1": ("sbuf", [128, 2 * C], f32), "g3": ("sbuf", [128, 2 * C], f32), "d0": ("sbuf", [128, 3 * C], f32), "d1": ("sbuf", [128, 3 * C], b16),
+    "kk": ("sbuf", [128, C], f32), "gg": ("sbuf", [128, C], f32), "dd": ("sbuf", [128, C], f32), "ow": ("sbuf", [128, C], f32),
+    "sc": ("sbuf", [128, 2 * C], i32), "mp": ("sbuf", [128, 2 * C], f32), "sc2": ("sbuf", [128, 2 * C], i32),
     "mt": ("sbuf", [128, H], f32), "st": ("sbuf", [128, H], f32),
     "lrow": ("sbuf", [128, 2 * C], f32),
-    "zz": ("sbuf", [128, 4 * C], b16), "zt": ("sbuf", [128, 4 * C], b16), "ht": ("sbuf", [128, 4 * C], b16), "hs": ("sbuf", [128, 4 * H], b16),
+    "zz": ("sbuf", [128, 4 * C], b16), "zt": ("sbuf", [128, 4 * C], b16), "ht": ("sbuf", [128, 4 * C], b16), "hp": ("sbuf", [128, 4 * H], b16),
     "ys": ("sbuf", [128, C], f32),
-    "pb": ("psum", [128, 1024], f32), "pt": ("psum", [128, 512], f32), "pr": ("psum", [128, 2048], f32),
+    "ps": ("psum", [128, 4096], f32),
 }
-HOLD = 4 * C + 1
-XL, L2, K2, KE = 0, 72, 90, 108
+HOLD = 2 * C + 1
+L2, K2, KE, L3, K3 = 72, 90, 108, 126, 144
 for _r in range(3):
-    SCRATCH["lo%d" % _r] = ("sbuf", [128, 126], u16)
+    SCRATCH["lo%d" % _r] = ("sbuf", [128, 162], u16)
     SCRATCH["kin%d" % _r] = ("sbuf", [128, 36], u16)
     SCRATCH["mm%d" % _r] = ("sbuf", [128, 72], u16)
     SCRATCH["min%d" % _r] = ("sbuf", [128, 36], u16)
@@ -53,11 +53,12 @@ for _r in range(3):
     SCRATCH["qin%d" % _r] = ("sbuf", [128, H], q8)
     SCRATCH["sin%d" % _r] = ("sbuf", [128, H], u8)
 SCRATCH["hq"] = ("sbuf", [128, H // 2], q8)
-SCRATCH["hsc"] = ("sbuf", [128, H // 2], u8)
+SCRATCH["hs"] = ("sbuf", [128, H // 2], u8)
 SCRATCH["hk"] = ("sbuf", [128, 18], u16)
 SCRATCH["hm"] = ("sbuf", [128, 18], u16)
-SEMAPHORES = ["cv", "cs", "ct", "cg", "sent", "out", "hq", "hs", "hk", "hm"] + ["%s%d" % (n, r) for n in ("ak", "am", "aq") for r in range(3)] \
-    + ["ld%d" % i for i in range(8)] + ["ga%d" % i for i in range(6)]
+KINDS = [("hk", 36, "kin", "ak"), ("hm", 36, "min", "am"), ("hq", H, "qin", "aq"), ("hs", H, "sin", "aq")]
+SEMAPHORES = ["cv", "cs", "ct", "cg", "sent", "out", "hq", "hs", "hk", "hm"] + ["%s%d" % (n, r) for n in ("ak", "am", "aq", "ga") for r in range(3)] \
+    + ["ld%d" % i for i in range(8)]
 
 
 def handers(topo, core, dst):
@@ -86,18 +87,14 @@ def hand_on(g, core, T, topo):
             hs = handers(topo, a, b)
             if hs is None or core not in hs:
                 continue
-            j = hs.index(core)
-            n = len(topo.engines(a, core)) // len(hs)
-            w, mw = H // len(hs), 36 // len(hs)
-            c0 = j * w
-            g.wait_ge(T.sem["hk"], n)
-            done += send(g, T, topo, core, b, T["kin%d" % r][:, j * mw:j * mw + mw], T["hk"][:, 0:mw], "ak%d" % r)
-            g.wait_ge(T.sem["hm"], n)
-            done += send(g, T, topo, core, b, T["min%d" % r][:, j * mw:j * mw + mw], T["hm"][:, 0:mw], "am%d" % r)
-            g.wait_ge(T.sem["hq"], n)
-            done += send(g, T, topo, core, b, T["qin%d" % r][:, c0:c0 + w].bitcast(dt.uint8), T["hq"][:, 0:w].bitcast(dt.uint8), "aq%d" % r)
-            g.wait_ge(T.sem["hs"], n)
-            done += send(g, T, topo, core, b, T["sin%d" % r][:, c0:c0 + w], T["hsc"][:, 0:w], "aq%d" % r)
+            for kind, width, into, sem in KINDS:
+                w = width // len(hs)
+                c0 = hs.index(core) * w
+                out, in_ = T[into + str(r)][:, c0:c0 + w], T[kind][:, 0:w]
+                if kind == "hq":
+                    out, in_ = out.bitcast(dt.uint8), in_.bitcast(dt.uint8)
+                g.wait_ge(T.sem[kind], len(topo.engines(a, core)) // len(hs))
+                done += send(g, T, topo, core, b, out, in_, sem + str(r))
     if done:
         g.wait_ge(T.sem["sent"], done)
 
@@ -155,17 +152,13 @@ def rank_program(g, core, T, topo):
         fn = {"copy": lambda: e.tensor_copy(*args), "tt": lambda: e.tensor_tensor(*args), "ts": lambda: e.tensor_scalar(*args),
               "scan": lambda: e.tensor_tensor_scan(*args), "quant": lambda: e.quantize_mx(*args), "memset": lambda: e.memset(*args),
               "act": lambda: e.activation(*args, **kw), "mm": lambda: e.matmul_mx(*args, True, True), "iota": lambda: e.iota(*args, **kw),
-              "sel": lambda: e.affine_select(*args), "dma": lambda: e.dma_start(*args, **kw)}[name]
+              "dma": lambda: e.dma_start(*args, **kw)}[name]
         after(q, fn(), sem, inc, reads, writes)
 
     def load(q, i, out, in_, key):
         op(q, "dma", (out, in_), [], [key], sem="ld%d" % i, inc=16)
 
     expect, done = {}, [0]
-
-    def arrives(sem, n, key):
-        expect[sem] = n
-        lastw[key] = (sem, n, "far")
 
     def ship(r, kind, out, in_, width, sem, keys):
         before("g", keys, [])
@@ -175,7 +168,7 @@ def rank_program(g, core, T, topo):
             done[0] += send(g, T, topo, core, dst, out(slice(0, width)), in_(slice(0, width)), sem)
             return
         w, ts = width // len(hs), []
-        land = T[{"hs": "hsc"}.get(kind, kind)][:, 0:w]
+        land = T[kind][:, 0:w]
         if kind == "hq":
             land = land.bitcast(dt.uint8)
         for j, h in enumerate(hs):
@@ -189,12 +182,10 @@ def rank_program(g, core, T, topo):
 
     for r in range(3):
         p = T.cores[rank ^ MASK[r]]
-        hs = handers(topo, p, core)
-        n, _ = engines8(topo, p if hs is None else hs[0], core)
-        n *= 1 if hs is None else len(hs)
-        arrives("ak%d" % r, n, "kin%d" % r)
-        arrives("am%d" % r, n, "min%d" % r)
-        arrives("aq%d" % r, 2 * n, "qin%d" % r)
+        n = sum(engines8(topo, c, core)[0] for c in (handers(topo, p, core) or [p]))
+        for sem, times, key in (("ak", 1, "kin"), ("am", 1, "min"), ("aq", 2, "qin")):
+            expect[sem + str(r)] = n * times
+            lastw[key + str(r)] = (sem + str(r), n * times, "far")
 
     def send_k(r):
         ship(r, "hk", lambda c: T["kin%d" % r][:, c], lambda c: T["lo%d" % r][:, c.start + K2:c.stop + K2], 36, "ak%d" % r, ["k2_%d" % r, "ke_%d" % r])
@@ -205,6 +196,77 @@ def rank_program(g, core, T, topo):
     def send_h(r):
         ship(r, "hq", lambda c: T["qin%d" % r][:, c].bitcast(dt.uint8), lambda c: T["qh%d" % r][:, c].bitcast(dt.uint8), H, "aq%d" % r, ["qh%d" % r])
         ship(r, "hs", lambda c: T["sin%d" % r][:, c], lambda c: T["sh%d" % r][:, c], H, "aq%d" % r, ["qh%d" % r])
+
+    def bank(i, n):
+        return T.ps[:, 512 * i:512 * i + n]
+
+    def first(at, src, by, add, key):
+        op("v", "ts", (T.lo0[:, at:at + 18], T[src][:], by, add, A.mult, A.add), [src], [key + "_0"])
+
+    def lists():
+        for t in range(4):
+            op("s", "act", (T.lf[:, 18 * t:18 * t + 18], T.lk[:, 0:18], F.Copy), ["fl"], ["lf%d" % t], scale=4.0, bias=float(t))
+        op("s", "act", (T.lf[:, L2:L2 + 36], T.lk[:], F.Copy), ["fl", "fk0", "fk1"], ["lf4"], scale=2.0, bias=1.0)
+        op("s", "act", (T.lf[:, KE:KE + 18], T.lk[:, 18:36], F.Copy), ["fk0", "fk1"], ["lf5"], scale=2.0)
+        op("s", "act", (T.lf[:, L3:L3 + 36], T.lk[:], F.Copy), ["fl", "fk0", "fk1"], ["lf6"], scale=3.0, bias=2.0)
+
+    def convert(r):
+        op("v", "copy", (T["lo%d" % r][:], T.lf[:]), ["lf%d" % i for i in range(7)], ["%s_%d" % (n, r) for n in ("xl0", "xl1", "xl2", "xl3", "l2", "k2", "ke", "l3", "k3")])
+
+    def unpacker(b):
+        c = slice(128 * b, 128 * b + 128)
+        op("v", "quant", (T.qe[:, c], T.se[:, c], T.et[:, 3 - b:515 - b]), ["et"], ["qe%d" % b])
+
+    def holder(e):
+        op("s", "act", (T.cf[:, HOLD + e:HOLD + 2 * C:8], T.labc[:, 0:72], F.Identity), ["labc", "k8"], ["hold%d" % e], scale=0.0, bias=T.k8[:, e:e + 1])
+
+    hold, held = T.cf[:, HOLD:HOLD + 2 * C], ["cfz"] + ["hold%d" % e for e in range(0, 8, 2)]
+
+    def spread(i):
+        c, by = slice(128 * i, 128 * i + 128), T.ofu[:, 8 * i:8 * i + 8]
+        op("v", "copy", (T.qr[:, c].bitcast(dt.uint32), T.qu[:].bitcast(dt.uint32).indirect(by)), ["qu", "ofu"], ["qr%d" % i])
+        op("s", "act", (T.sr[:, c], T.su[:].indirect(by), F.Copy), ["qu", "ofu"], ["sr%d" % i])
+
+    def scores(h):
+        c, e = slice(H * h, H * h + H), slice(4 * H * h, 4 * H * h + 4 * H)
+        n = "ab"[h]
+        op("v", "quant", (T.qx[:, c], T.sx[:, c], T.xt[:, e]), ["X%d" % h], ["qx" + n])
+        op("t", "mm", (bank(4 + h, H), T.qr[:, 0:128], T.sr[:, 0:128], T.qx[:, c], T.sx[:, c]), ["qr0", "sr0", "qx" + n], ["ps%d" % (4 + h)])
+
+    def lay(h):
+        c, n = slice(H * h, H * h + H), "ab"[h]
+        op("v", "tt", (T.v0[:, 2 * H * h + 1:2 * H * h + 2 * H:2], bank(4 + h, H), T.hi[:, c], A.min), ["ps%d" % (4 + h), "hi", "v0z"], ["V0" + n])
+
+    def sign(h):
+        op("v", "ts", (T.sg[:, H * h:H * h + H], T.v0[:, 2 * H * h + 1:2 * H * h + 2 * H:2], 0.0, 0.5, A.is_gt, A.subtract), ["V0" + "ab"[h]], ["sg" + "ab"[h]])
+
+    def factor(h, q):
+        out, in_, by, keys = T.cf[:, 2 * H * h + 1:2 * H * h + 2 * H:2], T.sg[:, H * h:H * h + H], -2.0 * STATE * TAG, (["sg" + "ab"[h]], ["i1" + "ab"[h]])
+        if q == "s":
+            op("s", "act", (out, in_, F.Copy), *keys, scale=by)
+        else:
+            op("v", "ts", (out, in_, by, None, A.mult), *keys)
+
+    def xl(r, t, q):
+        out, in_, keys = T.zz[:, t:4 * C:4], T.xt[:].indirect(T["lo%d" % r][:, 18 * t:18 * t + 18]), (["X0", "X1", "xl%d_%d" % (t, r)], ["zz%d" % t])
+        if q == "s":
+            op("s", "act", (out, in_, F.Copy), *keys)
+        else:
+            op("v", "copy", (out, in_), *keys)
+
+    zk = ["zz%d" % t for t in range(4)]
+
+    def differences(r):
+        l, k = (T.lk, T.lk) if r else (T.glt, T.gkt)
+        at = 18 if r else 0
+        op("v", "tt", (T.df[:, 0:9], k[:, at + 9:at + 18], l[:, 0:9], A.subtract), ["fl", "fk1"], ["df0"])
+        op("v", "tt", (T.df[:, 9:18], k[:, at:at + 9], l[:, 9:18], A.subtract), ["fl", "fk0"], ["df1"])
+
+    def offsets(row, low, out, okey, between=None):
+        op("v", "ts", (T[low][:], T[row][:, 7:2 * C:8], 2047, None, A.bitwise_and), [row], [low])
+        if between:
+            between()
+        op("v", "copy", (out[:], T[low][:]), [low], [okey])
 
     imprecise = {"allow_small_or_imprecise_dtypes": True}
     load("y", 0, T.gkt[:], T.gk[:], "gkt")
@@ -218,192 +280,125 @@ def rank_program(g, core, T, topo):
     op("g", "iota", (T.e16[:], [[0, 2], [1, 8]], 0, 0), [], ["e16"], **imprecise)
     op("g", "iota", (T.labc[:], [[4, C]], 0, 0), [], ["labc"], **imprecise)
     op("g", "iota", (T.ofi[:], [[1, 2], [16, 8]], 0, 0), [], ["ofi"])
+    op("g", "iota", (T.c16[:], [[0, 9], [1, 16]], 0, 0), [], ["c16"], **imprecise)
     op("g", "iota", (T.v0[:, 0:2 * C:2], [[0, C]], 0, 0), [], ["v0z"], **imprecise)
-    op("v", "memset", (T.et[:], 1.0), [], ["et"])
-    op("g", "sel", (T.et[:], T.et[:], [[-1, 516]], A.is_equal, 0.0, 3, 4), ["et"], ["et"])
-    op("g", "dma", (T.vt[:], T.v[:]), [], ["vt"], sem="ld7", inc=16)
+    op("g", "iota", (T.d0[:, 0:3 * C:3], [[0, C]], 0, 0), [], ["d0z"], **imprecise)
+    load("g", 7, T.vt[:], T.v[:], "vt")
+    op("v", "memset", (T.et[:], 0.0), [], ["et"])
     op("v", "ts", (T.pa[:, 1:2], T.pi[:, 1:2], 3, None, A.bitwise_and), ["pi"], ["pa1"])
     op("v", "ts", (T.pa[:, 2:3], T.pi[:, 2:3], 12, 1, A.bitwise_and, A.logical_shift_right), ["pi"], ["pa2"])
     op("v", "ts", (T.pa[:, 0:1], T.pi[:, 0:1], 15, None, A.bitwise_and), ["pi"], ["pa0"])
+    op("v", "ts", (T.pf[:, 4:5], T.pa[:, 1:2], U, SET * TAG, A.mult, A.add), ["pa1"], ["pf4"])
+    op("v", "ts", (T.pf[:, 3:4], T.pi[:, 3:4], -4.0, None, A.mult), ["pi"], ["pf3"])
     op("v", "copy", (T.pf[:, 0:3], T.pa[:, 0:3]), ["pa0", "pa1", "pa2"], ["pf"])
     op("v", "memset", (T.cf[:, 0:HOLD + 2 * C:2], 0.0), [], ["cfz"])
-    op("v", "ts", (T.pf[:, 4:5], T.pf[:, 1:2], U, SET * TAG, A.mult, A.add), ["pf"], ["pf4"])
     op("v", "ts", (T.r16[:], T.e16[:], T.pf[:, 2:3], BIG, A.is_equal, A.mult), ["e16", "pf"], ["r16"])
+    op("v", "ts", (T.up[:], T.e16[:, 0:4], 2.0 ** 59, 2.0 ** 59, A.mult, A.mult), ["e16"], ["up"])
     op("v", "copy", (T.ofu[:], T.ofi[:]), ["ofi"], ["ofu"])
     op("v", "ts", (T.r8[:], T.r16[:, 8:16], -2.0, None, A.mult), ["r16"], ["r8"])
+    op("v", "ts", (T.mask16[:], T.c16[:], T.pf[:, 0:1], -1e28, A.not_equal, A.mult), ["c16", "pf"], ["mask16"])
     op("v", "tt", (T.k8[:], T.r8[:], T.r16[:, 6:14], A.add), ["r8", "r16"], ["k8"])
+    op("s", "act", (T.d1[:, 1:3 * C:3], T.et[:, 0:C], F.Copy), ["et"], ["d1z"])
+    op("s", "act", (T.d1[:, 2:3 * C:3], T.et[:, 0:C], F.Copy), ["et"], ["d1s"], bias=SHIFT * T1)
     op("s", "act", (T.hi[:], T.labc[:], F.Identity), ["labc", "pf4"], ["hi"], scale=U, bias=T.pf[:, 4:5])
+    op("s", "act", (T.ea[:], T.labc[:, 0:128], F.Abs), ["labc", "pf3"], ["ea"], bias=T.pf[:, 3:4])
     op("s", "act", (T.own[:], T.hi[:], F.Copy), ["hi"], ["own"], bias=(OWN - SET) * TAG)
-    for e in range(0, 8, 2):
-        op("s", "act", (T.cf[:, HOLD + e:HOLD + 2 * C:8], T.labc[:, 0:72], F.Identity), ["labc", "k8"], ["hold%d" % e], scale=0.0, bias=T.k8[:, e:e + 1])
-    hold, held = T.cf[:, HOLD:HOLD + 2 * C], ["cfz"] + ["hold%d" % e for e in range(0, 8, 2)]
-
-    def lkeys(r):
-        return ["xl%d_%d" % (t, r) for t in range(4)] + ["l2_%d" % r, "k2_%d" % r, "ke_%d" % r]
-
-    def lists(r):
-        for t in range(4):
-            op("s", "act", (T.lf[:, 18 * t:18 * t + 18], T.lk[:, 0:18], F.Copy), ["fl"], ["lf%d" % t], scale=4.0, bias=float(t))
-        op("s", "act", (T.lf[:, L2:L2 + 18], T.lk[:, 0:18], F.Copy), ["fl"], ["lf4"], scale=2.0, bias=1.0)
-        for i, (at, add) in enumerate(((K2, 1.0), (KE, 0.0))):
-            op("s", "act", (T.lf[:, at:at + 9], T.lk[:, 27:36], F.Copy), ["fk"], ["lf%d" % (5 + 2 * i)], scale=2.0, bias=add)
-            op("s", "act", (T.lf[:, at + 9:at + 18], T.lk[:, 18:27], F.Copy), ["fk"], ["lf%d" % (6 + 2 * i)], scale=2.0, bias=add)
-
-    def convert(r):
-        op("v", "copy", (T["lo%d" % r][:], T.lf[:]), ["lf%d" % i for i in range(9)], lkeys(r))
-
-    op("v", "ts", (T.lo0[:, K2:K2 + 18], T.gkt[:], 2.0, 1.0, A.mult, A.add), ["gkt"], ["k2_0"])
-    op("v", "ts", (T.lo0[:, KE:KE + 18], T.gkt[:], 2.0, None, A.mult), ["gkt"], ["ke_0"])
-    send_k(0)
-    op("g", "iota", (T.c16[:], [[0, 9], [1, 16]], 0, 0), [], ["c16"], **imprecise)
-    op("v", "ts", (T.lo0[:, L2:L2 + 18], T.glt[:], 2.0, 1.0, A.mult, A.add), ["glt"], ["l2_0"])
+    op("s", "act", (T.et[:, 3:515:4], T.ea[:], F.Relu), ["ea", "d1z", "d1s"], ["et"], scale=-1.0, bias=1.0)
+    op("s", "act", (T.rs16[:], T.c16[:], F.Sign), ["c16"], ["rs16"])
     for t in range(4):
-        op("v", "ts", (T.lo0[:, 18 * t:18 * t + 18], T.glt[:], 4.0, float(t), A.mult, A.add), ["glt"], ["xl%d_0" % t])
+        first(18 * t, "glt", 4.0, float(t), "xl%d" % t)
     op("v", "quant", (T.qu[:], T.su[:], T.ut[:]), ["ut"], ["qu"])
-    op("v", "copy", (T.qr[:].bitcast(dt.uint32), T.qu[:].bitcast(dt.uint32).indirect(T.ofu[:])), ["qu", "ofu"], ["qr"])
-    op("s", "act", (T.sr[:], T.su[:].indirect(T.ofu[:]), F.Copy), ["qu", "ofu"], ["sr"])
-
-    def scores(h):
-        c, e = slice(H * h, H * h + H), slice(4 * H * h, 4 * H * h + 4 * H)
-        n = "ab"[h]
-        op("v", "quant", (T.qx[:, c], T.sx[:, c], T.xt[:, e]), ["X%d" % h], ["qx" + n])
-        op("t", "mm", (T.pb[:, 512 * h:512 * h + H], T.qr[:, 0:128], T.sr[:, 0:128], T.qx[:, c], T.sx[:, c]), ["qr", "sr", "qx" + n], ["pb" + n])
-        if h == 0:
-            op("t", "mm", (T.pt[:, 0:H], T.qr[:, 128:256], T.sr[:, 128:256], T.qx[:, c], T.sx[:, c]), ["qr", "sr", "qx" + n], ["pt"])
-
-    def lay(h):
-        c, odd, n = slice(H * h, H * h + H), slice(2 * H * h + 1, 2 * H * h + 2 * H, 2), "ab"[h]
-        op("v", "tt", (T.v0[:, odd], T.pb[:, 512 * h:512 * h + H], T.hi[:, c], A.min), ["pb" + n, "hi", "v0z"], ["V0" + n])
-
-    def sign(h):
-        n = "ab"[h]
-        op("s", "act", (T.sg[:, H * h:H * h + H], T.v0[:, 2 * H * h + 1:2 * H * h + 2 * H:2], F.Sign), ["V0" + n], ["sg" + n], bias=-TAG)
-
-    def factor(t, h, q="s"):
-        n, at, by = "ab"[h], 2 * C * (t - 1) + 2 * H * h, -STATE[t - 1] * TAG
-        out, in_ = T.cf[:, at + 1:at + 2 * H:2], T.sg[:, H * h:H * h + H]
-        if q == "s":
-            op("s", "act", (out, in_, F.Copy), ["sg" + n], ["i%d%s" % (t, n)], scale=by)
-        else:
-            op("v", "ts", (out, in_, by, None, A.mult), ["sg" + n], ["i%d%s" % (t, n)])
-
-    def xl(r, t, a, b):
-        op("s", "act", (T.zz[:, 64 * a + t:64 * b:4], T.xt[:].indirect(T["lo%d" % r][:, 18 * t + a:18 * t + b]), F.Copy), ["X0", "X1", "xl%d_%d" % (t, r)],
-           [k + str(t) for k, (c, d) in (("zA", (0, 10)), ("zB", (10, 18))) if a <= c and d <= b])
-
-    def add_x(i, a, b, key):
-        e, keys = slice(64 * a, 64 * b), [key + str(t) for t in range(4)]
-        op("g", "dma", (T.zz[:, e], T.xt[:, e]), ["X0", "X1"] + keys, keys, sem="ga%d" % i, inc=16, accum_op=A.add)
-
-    zk = [k + str(t) for k in ("zA", "zB") for t in range(4)]
-
-    def unpacker(b):
-        c = slice(128 * b, 128 * b + 128)
-        op("v", "quant", (T.qe[:, c], T.se[:, c], T.et[:, 3 - b:515 - b]), ["et"], ["qe%d" % b])
-
-    def offsets(row, key, whole, low, out, okey):
-        op("v", "ts", (T[whole][:], row[:, 7:2 * C:8], 2.0 ** 59, 2.0 ** 59, A.mult, A.mult), [key], [whole])
-        op("v", "ts", (T[low][:], T[whole][:], 2047, None, A.bitwise_and), [whole], [low])
-        op("v", "copy", (out[:], T[low][:]), [low], [okey])
-
+    first(K2, "gkt", 2.0, 1.0, "k2")
+    spread(0)
     scores(1)
+    first(KE, "gkt", 2.0, 0.0, "ke")
+    send_k(0)
+    first(L2, "glt", 2.0, 1.0, "l2")
+    spread(1)
     for r in range(3):
         rs = str(r)
         lo = T["lo" + rs]
-        byl, byk = lo[:, L2:L2 + 18], lo[:, K2:K2 + 18]
+        byl, byk, wk = lo[:, L2:L2 + 18], lo[:, K2:K2 + 18], ["V0a", "V0b", "v0z"]
         scores(0)
+        op("t", "mm", (bank(6, H), T.qr[:, 128:256], T.sr[:, 128:256], T.qx[:, 0:H], T.sx[:, 0:H]), ["qr1", "sr1", "qxa"], ["ps6"])
         if r == 0:
             lay(1)
-            xl(r, 0, 0, 18)
             sign(1)
-            factor(1, 1)
-        else:
-            op("v", "tt", (T.df[:], T.lk[:, 18:36], T.lk[:, 0:18], A.subtract), ["fl", "fk"], ["df"])
-            xl(r, 0, 0, 18)
+        for t in range(4):
+            xl(r, t, "sssv"[t])
+        op("g", "dma", (T.zz[:], T.xt[:]), ["X0", "X1"] + zk, zk, sem="ga" + rs, inc=16, accum_op=A.add)
         lay(0)
-        xl(r, 1, 0, 18)
-        for t in range(3):
-            win, wk = T["v%d" % t], (["V0a", "V0b", "v0z"] if t == 0 else ["V%d" % t])
-            own, ok = (T.own[:], "own") if t == 0 else (T["g%d" % t][:, 1:2 * C:2], "m%d" % t)
-            kk, gg = (T.g3[:, 0:2 * C:2], T.g3[:, 1:2 * C:2]) if t == 2 else (T.kk[:], T.gg[:])
-            kn, gn = ("kk3", "gg3") if t == 2 else ("kk", "gg")
-            op("v", "tt", (kk, win[:].indirect(byk), own, A.max), wk + ["k2_" + rs, ok], [kn])
-            op("s", "act", (gg, win[:].indirect(byl), F.Copy), wk + ["l2_" + rs], [gn], bias=LIFT[t] * TAG)
-            if t == 2:
-                if r == 0:
-                    unpacker(0)
-                break
-            op("v", "tt", (T.dd[:], win[:].indirect(byl), T.kk[:], A.subtract), wk + ["l2_" + rs, "kk"], ["dd"])
-            if t == 0:
-                sign(0)
-            else:
-                factor(2, 0)
-                if r == 0:
-                    factor(2, 1)
-            d1 = T["g%d" % (t + 1)]
-            op("s", "act", (d1[:, 0:2 * C:2], T.dd[:], F.Sign), ["dd"], ["s%d" % (t + 1)], bias=-CUT[t] * TAG)
-            op("v", "tt", (d1[:, 1:2 * C:2], T.kk[:], T.gg[:], A.max), ["kk", "gg"], ["m%d" % (t + 1)])
-            if t == 0:
-                factor(1, 0)
-                for i, (a, b, key) in enumerate(((0, 10, "zA"), (10, 18, "zB"))):
-                    xl(r, 2, a, b)
-                    xl(r, 3, a, b)
-                    add_x(2 * r + i, a, b, key)
-            i1 = "i%d" % (t + 1)
-            op("v", "scan", (T["v%d" % (t + 1)][:], T.cf[:, 2 * C * t:2 * C * t + 2 * C], d1[:], 0.0, A.mult, A.add),
-               [i1 + "a", i1 + "b", "cfz", "s%d" % (t + 1), "m%d" % (t + 1)], ["V%d" % (t + 1)])
+        op("v", "tt", (T.kk[:], T.v0[:].indirect(byk), T.own[:], A.max), wk + ["k2_" + rs, "own"], ["kk"])
+        op("s", "act", (T.gg[:], T.v0[:].indirect(byl), F.Copy), wk + ["l2_" + rs], ["gg"], bias=LIFT[0] * TAG)
+        sign(0)
+        op("v", "tt", (T.dd[:], T.v0[:].indirect(byl), T.kk[:], A.subtract), wk + ["l2_" + rs, "kk"], ["dd"])
+        factor(0, "s")
+        op("s", "act", (T.g1[:, 0:2 * C:2], T.dd[:], F.Sign), ["dd"], ["s1"], bias=-CUT * TAG)
+        op("v", "tt", (T.g1[:, 1:2 * C:2], T.kk[:], T.gg[:], A.max), ["kk", "gg"], ["m1"])
+        if r == 0:
+            factor(1, "v")
+        op("s", "act", (T.ow[:], T.g1[:, 1:2 * C:2], F.Copy), ["m1"], ["ow"], scale=-1.0, bias=-SINK * TAG)
+        op("s", "act", (T.d0[:, 1:3 * C:3], T.sg[:], F.Copy), ["sga", "sgb", "up"], ["d0s"], scale=T.up[:, 2:3])
+        op("v", "scan", (T.v1[:], T.cf[:, 0:2 * C], T.g1[:], 0.0, A.mult, A.add), ["i1a", "i1b", "cfz", "s1", "m1"], ["V1"])
+        if r == 0:
+            first(L3, "glt", 3.0, 2.0, "l3")
+        op("s", "act", (T.v0[:, 1:2 * C:2], T.v1[:, 1:2 * C:2], F.Copy), ["V1"], ["V0a", "V0b"], bias=LIFT[1] * TAG)
+        op("v", "tt", (T.kk[:], T.v1[:].indirect(byk), T.ow[:], A.max), ["V1", "k2_" + rs, "ow"], ["kk"])
+        op("v", "tt", (T.mt[:], bank(6, H), T.mask16[:], A.is_lt), ["ps6", "mask16"], ["mt"])
+        op("v", "tt", (T.d0[:, 2:3 * C:3], T.v0[:].indirect(byl), T.kk[:], A.max), wk + ["l2_" + rs, "kk"], ["mx"])
+        op("s", "act", (T.d1[:, 0:3 * C:3], T.kk[:], F.Sign), ["kk"], ["b1"])
+        if r == 0:
+            first(K3, "gkt", 3.0, 2.0, "k3")
+        op("s", "act", (T.ow[:], T.d0[:, 2:3 * C:3], F.Abs), ["mx", "up"], ["ow"], scale=T.up[:, 1:2])
+        op("v", "scan", (T.v2[:], T.d0[:], T.d1[:], 0.0, A.mult, A.add), ["d0z", "d0s", "mx", "d1z", "d1s", "b1"], ["V2"])
+        if r == 0:
+            for e in range(0, 8, 2):
+                holder(e)
+            unpacker(0)
+        op("v", "tt", (T.g3[:, 0:2 * C:2], T.v2[:].indirect(lo[:, K3:K3 + 18]), T.ow[:], A.max), ["V2", "k3_" + rs, "ow"], ["kk3"])
+        op("s", "act", (T.g3[:, 1:2 * C:2], T.v2[:].indirect(lo[:, L3:L3 + 18]), F.Copy), ["V2", "l3_" + rs], ["gg3"], bias=LIFT[2] * T1)
+        op("v", "scan", (T.st[:], T.rs16[:], T.mt[:], 0.0, A.mult, A.add), ["rs16", "mt"], ["st"])
         op("v", "scan", (T.sc[:], hold, T.g3[:], 0.0, A.add, A.max), held + ["kk3", "gg3"], ["sc"])
         op("s", "act", (T.mp[:, 1:2 * C:2], T.g3[:].indirect(T["kin" + rs][:, 0:18]), F.Copy), ["kk3", "gg3", "kin" + rs], ["mp1"])
         op("s", "act", (T.mp[:, 0:2 * C:2], T.g3[:].indirect(T["kin" + rs][:, 18:36]), F.Copy), ["kk3", "gg3", "kin" + rs], ["mp0"])
-        offsets(T.sc, "sc", "oi", "oa", T.oo, "oo")
+        if r == 0:
+            unpacker(1)
+        offsets("sc", "oa", T.oo, "oo", (lambda: unpacker(2)) if r == 0 else None)
         op("v", "ts", (T.zt[:, 0:576], T.zz[:].indirect(T.oo[:, 0:36]), 0.5, None, A.mult), zk + ["oo"], ["zt0"])
         op("s", "act", (T.zt[:, 576:1152], T.zz[:].indirect(T.oo[:, 36:72]), F.Copy), zk + ["oo"], ["zt1"], scale=0.5)
         if r == 0:
-            op("s", "act", (T.rs16[:], T.c16[:], F.Sign), ["c16"], ["rs16"])
-            op("s", "act", (T.mt[:], T.c16[:], F.Abs), ["c16", "pf"], ["mt"], scale=-1.0, bias=T.pf[:, 0:1])
-            op("s", "act", (T.mask16[:], T.mt[:], F.Copy), ["mt"], ["mask16"], scale=-1e28)
+            unpacker(3)
         op("v", "quant", (T.qz[:], T.sz[:], T.zt[:]), ["zt0", "zt1"], ["qz"])
         for b in range(4):
-            op("t", "mm", (T.pr[:, 512 * b:512 * b + C], T.qw[:, 128 * b:128 * b + 128], T.sw[:, 128 * b:128 * b + 128], T.qz[:], T.sz[:]), ["qw", "sw", "qz"], ["pr%d" % b])
+            op("t", "mm", (bank(b, C), T.qw[:, 128 * b:128 * b + 128], T.sw[:, 128 * b:128 * b + 128], T.qz[:], T.sz[:]), ["qw", "sw", "qz"], ["ps%d" % b])
         op("v", "scan", (T.sc2[:], hold, T.mp[:], 0.0, A.add, A.max), held + ["mp0", "mp1"], ["sc2"])
-        offsets(T.sc2, "sc2", "mi", "ma", T["mm" + rs], "mm" + rs)
+        offsets("sc2", "ma", T["mm" + rs], "mm" + rs)
         send_m(r)
+        differences(r)
         for b in range(4):
-            src, dst = T.pr[:, 512 * b:512 * b + C], T.ht[:, b:4 * C:4]
+            src, dst, keys = bank(b, C), T.ht[:, b:4 * C:4], (["ps%d" % b], ["h%d" % b])
             if b == 3:
-                op("v", "ts", (dst, src, 0.03125, None, A.mult), ["pr%d" % b], ["h%d" % b])
+                op("v", "ts", (dst, src, 0.03125, None, A.mult), *keys)
             else:
-                op("s", "act", (dst, src, F.Copy), ["pr%d" % b], ["h%d" % b], scale=0.03125)
-        hk = ["h0", "h1", "h2", "h3"]
-        op("v", "copy", (T.hs[:, 0:288], T.ht[:].indirect(T["mm" + rs][:, 0:18])), hk + ["mm" + rs], ["hs0"])
-        op("s", "act", (T.hs[:, 288:576], T.ht[:].indirect(T["mm" + rs][:, 18:36]), F.Copy), hk + ["mm" + rs], ["hs1"])
-        if r == 0:
-            unpacker(1)
-        op("v", "quant", (T["qh" + rs][:], T["sh" + rs][:], T.hs[:]), ["hs0", "hs1"], ["qh" + rs])
+                op("s", "act", (dst, src, F.Copy), *keys, scale=0.03125)
+        hk = ["h%d" % b for b in range(4)]
+        op("v", "copy", (T.hp[:, 0:16 * HV], T.ht[:].indirect(T["mm" + rs][:, 0:HV])), hk + ["mm" + rs], ["hp0"])
+        op("s", "act", (T.hp[:, 16 * HV:576], T.ht[:].indirect(T["mm" + rs][:, HV:36]), F.Copy), hk + ["mm" + rs], ["hp1"])
+        op("v", "quant", (T["qh" + rs][:], T["sh" + rs][:], T.hp[:]), ["hp0", "hp1"], ["qh" + rs])
         send_h(r)
-        if r == 0:
-            unpacker(2)
-            unpacker(3)
-            op("v", "tt", (T.df[:, 0:9], T.gkt[:, 9:18], T.glt[:, 0:9], A.subtract), ["glt", "gkt"], ["df"])
-            op("v", "tt", (T.df[:, 9:18], T.gkt[:, 0:9], T.glt[:, 9:18], A.subtract), ["glt", "gkt"], ["df1"])
-        op("v", "tt", (T.mt[:], T.pt[:, 0:H], T.mask16[:], A.is_lt), ["pt", "mask16"], ["mt"])
-        op("v", "scan", (T.st[:], T.rs16[:], T.mt[:], 0.0, A.mult, A.add), ["rs16", "mt"], ["st"])
-        op("v", "tt", (T.dt2[:, 0:9], T.df[:, 0:9], T.st[:, 15:H:16], A.mult), ["df", "st"], ["dt0"])
-        op("v", "tt", (T.dt2[:, 9:18], T.df[:, 9:18], T.st[:, 15:H:16], A.mult), ["df", "df1", "st"], ["dt1"])
-        if r == 0:
-            op("v", "tt", (T.lk[:, 18:27], T.gkt[:, 9:18], T.dt2[:, 0:9], A.subtract), ["gkt", "dt0"], ["fk0"])
-            op("v", "tt", (T.lk[:, 27:36], T.gkt[:, 0:9], T.dt2[:, 9:18], A.subtract), ["gkt", "dt1", "fk0"], ["fk"])
-        else:
-            op("v", "tt", (T.lk[:, 18:36], T.lk[:, 18:36], T.dt2[:], A.subtract), ["fk", "dt0", "dt1"], ["fk"])
-        op("v", "tt", (T.lk[:, 0:18], (T.lk[:, 0:18] if r else T.glt[:]), T.dt2[:], A.add), ["fl", "glt", "dt0", "dt1"], ["fl"])
+        l, k, at = (T.lk, T.lk, 18) if r else (T.glt, T.gkt, 0)
+        op("v", "tt", (T.dt2[:, 0:9], T.df[:, 0:9], T.st[:, 15:H:16], A.mult), ["df0", "st"], ["dt0"])
+        op("v", "tt", (T.dt2[:, 9:18], T.df[:, 9:18], T.st[:, 15:H:16], A.mult), ["df1", "st"], ["dt1"])
+        op("v", "tt", (T.lk[:, 27:36], k[:, at + 9:at + 18], T.dt2[:, 0:9], A.subtract), ["dt0", "fk1"], ["fk1"])
+        op("v", "tt", (T.lk[:, 0:18], l[:, 0:18], T.dt2[:], A.add), ["fl", "dt0", "dt1"], ["fl"])
+        op("v", "tt", (T.lk[:, 18:27], k[:, at:at + 9], T.dt2[:, 9:18], A.subtract), ["dt1", "fk0"], ["fk0"])
         if r < 2:
-            lists(r + 1)
+            lists()
         else:
-            op("v", "copy", (T.kf[:, 0:18], T.lk[:, 0:18]), ["fl"], ["kf0"])
-            op("v", "copy", (T.kf[:, 18:27], T.lk[:, 27:36]), ["fk"], ["kf1"])
-            op("v", "copy", (T.kf[:, 27:36], T.lk[:, 18:27]), ["fk"], ["kf2"])
-            op("s", "act", (T.lrow[:], T.labc[:].indirect(T.kf[:]), F.Copy), ["labc", "kf0", "kf1", "kf2"], ["lrow"], scale=0.25)
+            op("v", "copy", (T.kf[:], T.lk[:]), ["fl", "fk0", "fk1"], ["kf"])
+            op("s", "act", (T.lrow[:], T.labc[:].indirect(T.kf[:]), F.Copy), ["labc", "kf"], ["lrow"], scale=0.25)
             op("y", "dma", (T.lr[:], T.lrow[0:128:16, :]), ["lrow"], ["lr"], sem="out", inc=16)
+        if r == 1:
             op("v", "quant", (T.qv[:], T.sv[:], T.vt[:]), ["vt"], ["qv"])
         op("v", "tt", (T.xt[:, 576:1152], T.ht[:].indirect(T["min" + rs][:]), T.xt[:, 576:1152], A.add), hk + ["min" + rs, "X1"], ["X1"])
         if r < 2:
@@ -412,15 +407,14 @@ def rank_program(g, core, T, topo):
             send_k(r + 1)
             lay(1)
             sign(1)
-            factor(1, 1)
-            factor(2, 1)
+            factor(1, "s")
         else:
             output(op, T, 1)
         for b in range(4):
-            op("t", "mm", (T.pr[:, 512 * b:512 * b + H], T.qe[:, 128 * b:128 * b + 128], T.se[:, 128 * b:128 * b + 128], T["qin" + rs][:], T["sin" + rs][:]),
-               ["qe%d" % b, "qin" + rs], ["pr%d" % b])
+            op("t", "mm", (bank(b, H), T.qe[:, 128 * b:128 * b + 128], T.se[:, 128 * b:128 * b + 128], T["qin" + rs][:], T["sin" + rs][:]),
+               ["qe%d" % b, "qin" + rs], ["ps%d" % b])
         for b in range(4):
-            op("v", "tt", (T.xt[:, b:576:4], T.xt[:, b:576:4], T.pr[:, 512 * b:512 * b + H], A.add), ["pr%d" % b, "X0e%d" % b], ["X0e%d" % b])
+            op("v", "tt", (T.xt[:, b:576:4], T.xt[:, b:576:4], bank(b, H), A.add), ["ps%d" % b, "X0e%d" % b], ["X0e%d" % b])
     output(op, T, 0)
     for sem, n in sorted(count.items()) + sorted(expect.items()):
         if waited["g"].get(sem, 0) < n:
@@ -429,11 +423,11 @@ def rank_program(g, core, T, topo):
 
 
 def output(op, T, h):
-    n, c, e = "ab"[h], slice(H * h, H * h + H), slice(4 * H * h, 4 * H * h + 4 * H)
+    n, c, e, at = "ab"[h], slice(H * h, H * h + H), slice(4 * H * h, 4 * H * h + 4 * H), 512 * (4 + h)
     op("v", "quant", (T.qx[:, c], T.sx[:, c], T.xt[:, e]), ["X%d" % h], ["qx" + n])
-    op("t", "mm", (T.pb[:, 512 * h:512 * h + H], T.qv[:], T.sv[:], T.qx[:, c], T.sx[:, c]), ["qv", "qx" + n], ["pb" + n])
+    op("t", "mm", (T.ps[:, at:at + H], T.qv[:], T.sv[:], T.qx[:, c], T.sx[:, c]), ["qv", "qx" + n], ["ps%d" % (4 + h)])
     op("y", "dma", (T.oc[:, e], T.qx[:, c].bitcast(dt.uint8)), ["qx" + n], ["oc" + n], sem="out", inc=16)
     for k in range(4):
-        op("y", "dma", (T.osc[4 * k:4 * k + 4, c], T.sx[32 * k:32 * k + 4, c]), ["qx" + n], ["osc%s%d" % (n, k)], sem="out", inc=16)
-    op("v", "copy", (T.ys[:, c], T.pb[:, 512 * h:512 * h + H]), ["pb" + n], ["ys" + n])
+        op("ys"[k // 2], "dma", (T.osc[4 * k:4 * k + 4, c], T.sx[32 * k:32 * k + 4, c]), ["qx" + n], ["osc%s%d" % (n, k)], sem="out", inc=16)
+    op("v", "copy", (T.ys[:, c], T.ps[:, at:at + H]), ["ps%d" % (4 + h)], ["ys" + n])
     op("s", "dma", (T.y[:, c], T.ys[:, c]), ["ys" + n], ["y" + n], sem="out", inc=16)

@@ -6,11 +6,11 @@ C, H = 288, 144
 U = 2.0 ** -118
 T1 = 2048.0
 TAG = T1 * U
-OWN, SET, CUT, STATE = 2, 4, 1, 40
+OWN, SET, STATE = 2, 4, 40
 SINK, SHIFT = 24, 24
 LIFT = [1, 4, 24]
 BIG = 128 * T1
-HV = 20
+RUNS = ((0, 10), (10, 18))
 f32, b16, i32, u16, u8, q8 = "float32", "bfloat16", "int32", "uint16", "uint8", "float8_e4m3fn_x4"
 SCRATCH = {
     "xt": ("sbuf", [128, 4 * C], b16), "ut": ("sbuf", [128, 512], b16), "vt": ("sbuf", [128, 512], b16),
@@ -29,11 +29,12 @@ SCRATCH = {
     "mask16": ("sbuf", [128, H], f32), "rs16": ("sbuf", [128, H], f32),
     "hi": ("sbuf", [128, C], f32), "own": ("sbuf", [128, C], f32), "ofi": ("sbuf", [128, 16], i32), "ofu": ("sbuf", [128, 16], u16),
     "lk": ("sbuf", [128, 36], f32), "df": ("sbuf", [128, 18], f32), "dt2": ("sbuf", [128, 18], f32),
-    "lf": ("sbuf", [128, 162], f32), "kf": ("sbuf", [128, 36], u16),
+    "lf": ("sbuf", [128, 126], f32), "kf": ("sbuf", [128, 36], u16),
     "oo": ("sbuf", [128, 72], u16), "oa": ("sbuf", [128, 72], i32), "ma": ("sbuf", [128, 72], i32),
-    "sg": ("sbuf", [128, C], f32), "v0": ("sbuf", [128, 2 * C], f32), "v1": ("sbuf", [128, 2 * C], f32), "v2": ("sbuf", [128, 3 * C], f32),
-    "g1": ("sbuf", [128, 2 * C], f32), "g3": ("sbuf", [128, 2 * C], f32), "d0": ("sbuf", [128, 3 * C], f32), "d1": ("sbuf", [128, 3 * C], b16),
-    "kk": ("sbuf", [128, C], f32), "gg": ("sbuf", [128, C], f32), "dd": ("sbuf", [128, C], f32), "ow": ("sbuf", [128, C], f32),
+    "sg": ("sbuf", [128, 2 * C], f32), "v0": ("sbuf", [128, 2 * C], f32), "w0": ("sbuf", [128, 2 * C], f32), "v1": ("sbuf", [128, 2 * C], f32),
+    "v2": ("sbuf", [128, 3 * C], f32), "g1": ("sbuf", [128, 2 * C], f32), "g3": ("sbuf", [128, 2 * C], f32),
+    "d0": ("sbuf", [128, 3 * C], f32), "d1": ("sbuf", [128, 3 * C], b16),
+    "kk": ("sbuf", [128, C], f32), "nb": ("sbuf", [128, C], f32), "ow": ("sbuf", [128, C], f32),
     "sc": ("sbuf", [128, 2 * C], i32), "mp": ("sbuf", [128, 2 * C], f32), "sc2": ("sbuf", [128, 2 * C], i32),
     "mt": ("sbuf", [128, H], f32), "st": ("sbuf", [128, H], f32),
     "lrow": ("sbuf", [128, 2 * C], f32),
@@ -42,7 +43,7 @@ SCRATCH = {
     "ps": ("psum", [128, 4096], f32),
 }
 HOLD = 2 * C + 1
-L2, K2, KE, L3, K3 = 72, 90, 108, 126, 144
+L2, L3, K3, K2, KE = 72, 90, 108, 126, 144
 for _r in range(3):
     SCRATCH["lo%d" % _r] = ("sbuf", [128, 162], u16)
     SCRATCH["kin%d" % _r] = ("sbuf", [128, 36], u16)
@@ -206,12 +207,11 @@ def rank_program(g, core, T, topo):
     def lists():
         for t in range(4):
             op("s", "act", (T.lf[:, 18 * t:18 * t + 18], T.lk[:, 0:18], F.Copy), ["fl"], ["lf%d" % t], scale=4.0, bias=float(t))
-        op("s", "act", (T.lf[:, L2:L2 + 36], T.lk[:], F.Copy), ["fl", "fk0", "fk1"], ["lf4"], scale=2.0, bias=1.0)
-        op("s", "act", (T.lf[:, KE:KE + 18], T.lk[:, 18:36], F.Copy), ["fk0", "fk1"], ["lf5"], scale=2.0)
-        op("s", "act", (T.lf[:, L3:L3 + 36], T.lk[:], F.Copy), ["fl", "fk0", "fk1"], ["lf6"], scale=3.0, bias=2.0)
+        op("s", "act", (T.lf[:, L2:L2 + 18], T.lk[:, 0:18], F.Copy), ["fl"], ["lf4"], scale=2.0, bias=1.0)
+        op("s", "act", (T.lf[:, L3:L3 + 36], T.lk[:], F.Copy), ["fl", "fk0", "fk1"], ["lf5"], scale=3.0, bias=2.0)
 
     def convert(r):
-        op("v", "copy", (T["lo%d" % r][:], T.lf[:]), ["lf%d" % i for i in range(7)], ["%s_%d" % (n, r) for n in ("xl0", "xl1", "xl2", "xl3", "l2", "k2", "ke", "l3", "k3")])
+        op("v", "copy", (T["lo%d" % r][:, 0:K2], T.lf[:]), ["lf%d" % i for i in range(6)], ["%s_%d" % (n, r) for n in ("xl0", "xl1", "xl2", "xl3", "l2", "l3", "k3")])
 
     def unpacker(b):
         c = slice(128 * b, 128 * b + 128)
@@ -233,19 +233,30 @@ def rank_program(g, core, T, topo):
         op("v", "quant", (T.qx[:, c], T.sx[:, c], T.xt[:, e]), ["X%d" % h], ["qx" + n])
         op("t", "mm", (bank(4 + h, H), T.qr[:, 0:128], T.sr[:, 0:128], T.qx[:, c], T.sx[:, c]), ["qr0", "sr0", "qx" + n], ["ps%d" % (4 + h)])
 
+    def span(h, n, at):
+        a, b = ((0, H), (H, C), (0, C))[h]
+        return slice(n * a + at, n * b, n)
+
+    def names(key, h):
+        return [key + n for n in ("a", "b", "ab")[h]]
+
+    def runs(key):
+        return ["%s%d" % (key, a) for a, b in RUNS]
+
     def lay(h):
-        c, n = slice(H * h, H * h + H), "ab"[h]
-        op("v", "tt", (T.v0[:, 2 * H * h + 1:2 * H * h + 2 * H:2], bank(4 + h, H), T.hi[:, c], A.min), ["ps%d" % (4 + h), "hi", "v0z"], ["V0" + n])
+        op("v", "tt", (T.v0[:, span(h, 2, 1)], bank(4 + h, H), T.hi[:, span(h, 1, 0)], A.min), ["ps%d" % (4 + h), "hi", "v0z"], names("V0", h) + ["V0c"])
 
     def sign(h):
-        op("v", "ts", (T.sg[:, H * h:H * h + H], T.v0[:, 2 * H * h + 1:2 * H * h + 2 * H:2], 0.0, 0.5, A.is_gt, A.subtract), ["V0" + "ab"[h]], ["sg" + "ab"[h]])
+        op("v", "ts", (T.sg[:, span(h, 2, 1)], bank(4 + h, H), 0.0, 0.5, A.is_gt, A.subtract), ["ps%d" % (4 + h), "sgz"], names("sg", h))
 
-    def factor(h, q):
-        out, in_, by, keys = T.cf[:, 2 * H * h + 1:2 * H * h + 2 * H:2], T.sg[:, H * h:H * h + H], -2.0 * STATE * TAG, (["sg" + "ab"[h]], ["i1" + "ab"[h]])
-        if q == "s":
-            op("s", "act", (out, in_, F.Copy), *keys, scale=by)
-        else:
-            op("v", "ts", (out, in_, by, None, A.mult), *keys)
+    def lifted(h):
+        op("s", "act", (T.w0[:, span(h, 2, 1)], T.v0[:, span(h, 2, 1)], F.Copy), names("V0", h), names("w0", h), bias=LIFT[0] * TAG)
+
+    def factor(h):
+        op("s", "act", (T.cf[:, span(h, 2, 1)], T.sg[:, span(h, 2, 1)], F.Copy), names("sg", h), names("i1", h), scale=-4.0 * STATE * TAG)
+
+    def signed(h):
+        op("s", "act", (T.d0[:, span(h, 3, 1)], T.sg[:, span(h, 2, 1)], F.Copy), names("sg", h) + ["up"], names("d0", h), scale=T.up[:, 2:3])
 
     def xl(r, t, q):
         out, in_, keys = T.zz[:, t:4 * C:4], T.xt[:].indirect(T["lo%d" % r][:, 18 * t:18 * t + 18]), (["X0", "X1", "xl%d_%d" % (t, r)], ["zz%d" % t])
@@ -256,17 +267,14 @@ def rank_program(g, core, T, topo):
 
     zk = ["zz%d" % t for t in range(4)]
 
+    def add_x(r):
+        op("g", "dma", (T.zz[:], T.xt[:]), ["X0", "X1"] + zk, zk, sem="ga%d" % r, inc=16, accum_op=A.add)
+
     def differences(r):
         l, k = (T.lk, T.lk) if r else (T.glt, T.gkt)
         at = 18 if r else 0
-        op("v", "tt", (T.df[:, 0:9], k[:, at + 9:at + 18], l[:, 0:9], A.subtract), ["fl", "fk1"], ["df0"])
-        op("v", "tt", (T.df[:, 9:18], k[:, at:at + 9], l[:, 9:18], A.subtract), ["fl", "fk0"], ["df1"])
-
-    def offsets(row, low, out, okey, between=None):
-        op("v", "ts", (T[low][:], T[row][:, 7:2 * C:8], 2047, None, A.bitwise_and), [row], [low])
-        if between:
-            between()
-        op("v", "copy", (out[:], T[low][:]), [low], [okey])
+        op("v", "tt", (T.df[:, 0:9], k[:, at + 9:at + 18], l[:, 0:9], A.subtract), ["fl", "fk1", "glt", "gkt"], ["df0"])
+        op("v", "tt", (T.df[:, 9:18], k[:, at:at + 9], l[:, 9:18], A.subtract), ["fl", "fk0", "glt", "gkt"], ["df1"])
 
     imprecise = {"allow_small_or_imprecise_dtypes": True}
     load("y", 0, T.gkt[:], T.gk[:], "gkt")
@@ -274,16 +282,18 @@ def rank_program(g, core, T, topo):
     load("s", 2, T.ut[:], T.u[:], "ut")
     load("y", 3, T.xt[:, 576:1152], T.x[:, 576:1152], "X1")
     load("y", 4, T.xt[:, 0:576], T.x[:, 0:576], "X0")
+    before("y", parts(["X0", "X1"]), [])
     load("y", 5, T.qw[:].bitcast(dt.uint8), T.wc[:], "qw")
-    load("y", 6, T.sw[:], T.ws[:], "sw")
+    load("y", 6, T.vt[:], T.v[:], "vt")
     op("g", "iota", (T.pi[:], [[0, 4]], 0, 1), [], ["pi"])
     op("g", "iota", (T.e16[:], [[0, 2], [1, 8]], 0, 0), [], ["e16"], **imprecise)
     op("g", "iota", (T.labc[:], [[4, C]], 0, 0), [], ["labc"], **imprecise)
     op("g", "iota", (T.ofi[:], [[1, 2], [16, 8]], 0, 0), [], ["ofi"])
     op("g", "iota", (T.c16[:], [[0, 9], [1, 16]], 0, 0), [], ["c16"], **imprecise)
     op("g", "iota", (T.v0[:, 0:2 * C:2], [[0, C]], 0, 0), [], ["v0z"], **imprecise)
+    op("g", "iota", (T.w0[:, 0:2 * C:2], [[0, C]], 0, 0), [], ["w0z"], **imprecise)
     op("g", "iota", (T.d0[:, 0:3 * C:3], [[0, C]], 0, 0), [], ["d0z"], **imprecise)
-    load("g", 7, T.vt[:], T.v[:], "vt")
+    load("g", 7, T.sw[:], T.ws[:], "sw")
     op("v", "memset", (T.et[:], 0.0), [], ["et"])
     op("v", "ts", (T.pa[:, 1:2], T.pi[:, 1:2], 3, None, A.bitwise_and), ["pi"], ["pa1"])
     op("v", "ts", (T.pa[:, 2:3], T.pi[:, 2:3], 12, 1, A.bitwise_and, A.logical_shift_right), ["pi"], ["pa2"])
@@ -292,6 +302,7 @@ def rank_program(g, core, T, topo):
     op("v", "ts", (T.pf[:, 3:4], T.pi[:, 3:4], -4.0, None, A.mult), ["pi"], ["pf3"])
     op("v", "copy", (T.pf[:, 0:3], T.pa[:, 0:3]), ["pa0", "pa1", "pa2"], ["pf"])
     op("v", "memset", (T.cf[:, 0:HOLD + 2 * C:2], 0.0), [], ["cfz"])
+    op("v", "memset", (T.sg[:, 0:2 * C:2], 0.0), [], ["sgz"])
     op("v", "ts", (T.r16[:], T.e16[:], T.pf[:, 2:3], BIG, A.is_equal, A.mult), ["e16", "pf"], ["r16"])
     op("v", "ts", (T.up[:], T.e16[:, 0:4], 2.0 ** 59, 2.0 ** 59, A.mult, A.mult), ["e16"], ["up"])
     op("v", "copy", (T.ofu[:], T.ofi[:]), ["ofi"], ["ofu"])
@@ -307,6 +318,8 @@ def rank_program(g, core, T, topo):
     op("s", "act", (T.rs16[:], T.c16[:], F.Sign), ["c16"], ["rs16"])
     for t in range(4):
         first(18 * t, "glt", 4.0, float(t), "xl%d" % t)
+    holder(0)
+    holder(2)
     op("v", "quant", (T.qu[:], T.su[:], T.ut[:]), ["ut"], ["qu"])
     first(K2, "gkt", 2.0, 1.0, "k2")
     spread(0)
@@ -314,67 +327,104 @@ def rank_program(g, core, T, topo):
     first(KE, "gkt", 2.0, 0.0, "ke")
     send_k(0)
     first(L2, "glt", 2.0, 1.0, "l2")
-    spread(1)
     for r in range(3):
         rs = str(r)
         lo = T["lo" + rs]
-        byl, byk, wk = lo[:, L2:L2 + 18], lo[:, K2:K2 + 18], ["V0a", "V0b", "v0z"]
+        late = 0 if r else 2
+        wk, sk = ["V0a", "V0b", "V0c", "v0z"], ["sga", "sgb", "sgz"]
         scores(0)
-        op("t", "mm", (bank(6, H), T.qr[:, 128:256], T.sr[:, 128:256], T.qx[:, 0:H], T.sx[:, 0:H]), ["qr1", "sr1", "qxa"], ["ps6"])
         if r == 0:
             lay(1)
             sign(1)
-        for t in range(4):
-            xl(r, t, "sssv"[t])
-        op("g", "dma", (T.zz[:], T.xt[:]), ["X0", "X1"] + zk, zk, sem="ga" + rs, inc=16, accum_op=A.add)
-        lay(0)
-        op("v", "tt", (T.kk[:], T.v0[:].indirect(byk), T.own[:], A.max), wk + ["k2_" + rs, "own"], ["kk"])
-        op("s", "act", (T.gg[:], T.v0[:].indirect(byl), F.Copy), wk + ["l2_" + rs], ["gg"], bias=LIFT[0] * TAG)
+        xl(r, 0, "s")
+        xl(r, 1, "s")
+        if r:
+            xl(r, 3, "v")
         sign(0)
-        op("v", "tt", (T.dd[:], T.v0[:].indirect(byl), T.kk[:], A.subtract), wk + ["l2_" + rs, "kk"], ["dd"])
-        factor(0, "s")
-        op("s", "act", (T.g1[:, 0:2 * C:2], T.dd[:], F.Sign), ["dd"], ["s1"], bias=-CUT * TAG)
-        op("v", "tt", (T.g1[:, 1:2 * C:2], T.kk[:], T.gg[:], A.max), ["kk", "gg"], ["m1"])
+        lay(0)
+        op("v", "tt", (T.kk[:], T.v0[:].indirect(lo[:, K2:K2 + 18]), T.own[:], A.max), wk + ["k2_" + rs, "own"], runs("kk"))
+        op("s", "act", (T.nb[:], T.sg[:].indirect(lo[:, K2:K2 + 18]), F.Copy), sk + ["k2_" + rs], ["nb"], scale=-1.0)
+        lifted(late)
+        if r:
+            xl(r, 2, "s")
+            add_x(r)
+            factor(late)
+            signed(late)
+        else:
+            factor(late)
+            xl(r, 2, "s")
+            xl(r, 3, "s")
+            add_x(r)
+        op("v", "tt", (T.g1[:, 0:2 * C:2], T.sg[:].indirect(lo[:, L2:L2 + 18]), T.nb[:], A.min), sk + ["l2_" + rs, "nb"], ["s1"])
+        for a, b in RUNS:
+            op("v", "tt", (T.g1[:, 32 * a + 1:32 * b:2], T.w0[:].indirect(lo[:, L2 + a:L2 + b]), T.kk[:, 16 * a:16 * b], A.max),
+               ["kk%d" % a, "w0a", "w0b", "w0z", "l2_" + rs], ["m1%d" % a])
+        op("s", "act", (T.ow[:], T.g1[:, 1:2 * C:2], F.Copy), runs("m1"), ["ow"], scale=-1.0, bias=-SINK * TAG)
         if r == 0:
-            factor(1, "v")
-        op("s", "act", (T.ow[:], T.g1[:, 1:2 * C:2], F.Copy), ["m1"], ["ow"], scale=-1.0, bias=-SINK * TAG)
-        op("s", "act", (T.d0[:, 1:3 * C:3], T.sg[:], F.Copy), ["sga", "sgb", "up"], ["d0s"], scale=T.up[:, 2:3])
-        op("v", "scan", (T.v1[:], T.cf[:, 0:2 * C], T.g1[:], 0.0, A.mult, A.add), ["i1a", "i1b", "cfz", "s1", "m1"], ["V1"])
+            signed(late)
+        for a, b in RUNS:
+            e, odd = slice(32 * a, 32 * b), slice(32 * a + 1, 32 * b, 2)
+            op("v", "scan", (T.v1[:, e], T.cf[:, e], T.g1[:, e], 0.0, A.mult, A.add), ["i1a", "i1b", "cfz", "s1", "m1%d" % a], ["V1%d" % a])
+            op("s", "act", (T.v0[:, odd], T.v1[:, odd], F.Copy), ["V1%d" % a], ["V0c"] if a else ["V0a", "V0b"], bias=LIFT[1] * TAG)
         if r == 0:
             first(L3, "glt", 3.0, 2.0, "l3")
-        op("s", "act", (T.v0[:, 1:2 * C:2], T.v1[:, 1:2 * C:2], F.Copy), ["V1"], ["V0a", "V0b"], bias=LIFT[1] * TAG)
-        op("v", "tt", (T.kk[:], T.v1[:].indirect(byk), T.ow[:], A.max), ["V1", "k2_" + rs, "ow"], ["kk"])
-        op("v", "tt", (T.mt[:], bank(6, H), T.mask16[:], A.is_lt), ["ps6", "mask16"], ["mt"])
-        op("v", "tt", (T.d0[:, 2:3 * C:3], T.v0[:].indirect(byl), T.kk[:], A.max), wk + ["l2_" + rs, "kk"], ["mx"])
-        op("s", "act", (T.d1[:, 0:3 * C:3], T.kk[:], F.Sign), ["kk"], ["b1"])
+            spread(1)
+        op("t", "mm", (bank(6, H), T.qr[:, 128:256], T.sr[:, 128:256], T.qx[:, 0:H], T.sx[:, 0:H]), ["qr1", "sr1", "qxa"], ["ps6"])
+        for a, b in RUNS:
+            c = slice(16 * a, 16 * b)
+            op("v", "tt", (T.kk[:, c], T.v1[:].indirect(lo[:, K2 + a:K2 + b]), T.ow[:, c], A.max), runs("V1") + ["k2_" + rs, "ow"], ["kk%d" % a])
+            op("s", "act", (T.d1[:, 48 * a:48 * b:3], T.kk[:, c], F.Sign), ["kk%d" % a], ["b1%d" % a])
+        for a, b in RUNS:
+            op("v", "tt", (T.d0[:, 48 * a + 2:48 * b:3], T.v0[:].indirect(lo[:, L2 + a:L2 + b]), T.kk[:, 16 * a:16 * b], A.max), wk + ["l2_" + rs, "kk%d" % a], ["mx%d" % a])
         if r == 0:
             first(K3, "gkt", 3.0, 2.0, "k3")
-        op("s", "act", (T.ow[:], T.d0[:, 2:3 * C:3], F.Abs), ["mx", "up"], ["ow"], scale=T.up[:, 1:2])
-        op("v", "scan", (T.v2[:], T.d0[:], T.d1[:], 0.0, A.mult, A.add), ["d0z", "d0s", "mx", "d1z", "d1s", "b1"], ["V2"])
+        op("s", "act", (T.ow[:], T.d0[:, 2:3 * C:3], F.Abs), runs("mx") + ["up"], ["ow"], scale=T.up[:, 1:2])
+        for a, b in RUNS:
+            e = slice(48 * a, 48 * b)
+            op("v", "scan", (T.v2[:, e], T.d0[:, e], T.d1[:, e], 0.0, A.mult, A.add), ["d0z", "d0a", "d0b", "mx%d" % a, "d1z", "d1s", "b1%d" % a], ["V2%d" % a])
         if r == 0:
-            for e in range(0, 8, 2):
-                holder(e)
+            holder(4)
+            holder(6)
             unpacker(0)
-        op("v", "tt", (T.g3[:, 0:2 * C:2], T.v2[:].indirect(lo[:, K3:K3 + 18]), T.ow[:], A.max), ["V2", "k3_" + rs, "ow"], ["kk3"])
-        op("s", "act", (T.g3[:, 1:2 * C:2], T.v2[:].indirect(lo[:, L3:L3 + 18]), F.Copy), ["V2", "l3_" + rs], ["gg3"], bias=LIFT[2] * T1)
+        op("v", "tt", (T.mt[:], bank(6, H), T.mask16[:], A.is_lt), ["ps6", "mask16"], ["mt"])
+        for a, b in RUNS:
+            op("v", "tt", (T.g3[:, 32 * a:32 * b:2], T.v2[:].indirect(lo[:, K3 + a:K3 + b]), T.ow[:, 16 * a:16 * b], A.max), runs("V2") + ["k3_" + rs, "ow"], ["kk3%d" % a])
+            op("s", "act", (T.g3[:, 32 * a + 1:32 * b:2], T.v2[:].indirect(lo[:, L3 + a:L3 + b]), F.Copy), runs("V2") + ["l3_" + rs], ["gg3%d" % a], bias=LIFT[2] * T1)
+        for a, b in RUNS:
+            op("v", "scan", (T.sc[:, 32 * a:32 * b], T.cf[:, HOLD + 32 * a:HOLD + 32 * b], T.g3[:, 32 * a:32 * b], 0.0, A.add, A.max), held + ["kk3%d" % a, "gg3%d" % a], ["sc%d" % a])
+        gk = runs("kk3") + runs("gg3") + ["kin" + rs]
+        op("s", "act", (T.mp[:, 1:2 * C:2], T.g3[:].indirect(T["kin" + rs][:, 0:18]), F.Copy), gk, ["mp1"])
+        for a, b in RUNS:
+            op("v", "ts", (T.oa[:, 4 * a:4 * b], T.sc[:, 32 * a + 7:32 * b:8], 2047, None, A.bitwise_and), ["sc%d" % a], ["oa%d" % a])
+            if r == 0 and a == 0:
+                unpacker(1)
         op("v", "scan", (T.st[:], T.rs16[:], T.mt[:], 0.0, A.mult, A.add), ["rs16", "mt"], ["st"])
-        op("v", "scan", (T.sc[:], hold, T.g3[:], 0.0, A.add, A.max), held + ["kk3", "gg3"], ["sc"])
-        op("s", "act", (T.mp[:, 1:2 * C:2], T.g3[:].indirect(T["kin" + rs][:, 0:18]), F.Copy), ["kk3", "gg3", "kin" + rs], ["mp1"])
-        op("s", "act", (T.mp[:, 0:2 * C:2], T.g3[:].indirect(T["kin" + rs][:, 18:36]), F.Copy), ["kk3", "gg3", "kin" + rs], ["mp0"])
-        if r == 0:
-            unpacker(1)
-        offsets("sc", "oa", T.oo, "oo", (lambda: unpacker(2)) if r == 0 else None)
-        op("v", "ts", (T.zt[:, 0:576], T.zz[:].indirect(T.oo[:, 0:36]), 0.5, None, A.mult), zk + ["oo"], ["zt0"])
-        op("s", "act", (T.zt[:, 576:1152], T.zz[:].indirect(T.oo[:, 36:72]), F.Copy), zk + ["oo"], ["zt1"], scale=0.5)
+        for a, b in RUNS:
+            op("v", "copy", (T.oo[:, 4 * a:4 * b], T.oa[:, 4 * a:4 * b]), ["oa%d" % a], ["oo%d" % a])
+            if r == 0 and a == 0:
+                unpacker(2)
+        (a, b), (c, d) = RUNS
+        op("s", "act", (T.zt[:, 64 * a:64 * b], T.zz[:].indirect(T.oo[:, 4 * a:4 * b]), F.Copy), zk + ["oo%d" % a], ["zt%d" % a], scale=0.5)
+        op("v", "ts", (T.zt[:, 64 * c:64 * d], T.zz[:].indirect(T.oo[:, 4 * c:4 * d]), 0.5, None, A.mult), zk + ["oo%d" % c], ["zt%d" % c])
+        op("s", "act", (T.mp[:, 0:2 * C:2], T.g3[:].indirect(T["kin" + rs][:, 18:36]), F.Copy), gk, ["mp0"])
         if r == 0:
             unpacker(3)
-        op("v", "quant", (T.qz[:], T.sz[:], T.zt[:]), ["zt0", "zt1"], ["qz"])
+        for a, b in RUNS[::-1]:
+            op("v", "quant", (T.qz[:, 16 * a:16 * b], T.sz[:, 16 * a:16 * b], T.zt[:, 64 * a:64 * b]), ["zt%d" % a], ["qz%d" % a])
         for b in range(4):
-            op("t", "mm", (bank(b, C), T.qw[:, 128 * b:128 * b + 128], T.sw[:, 128 * b:128 * b + 128], T.qz[:], T.sz[:]), ["qw", "sw", "qz"], ["ps%d" % b])
+            op("t", "mm", (bank(b, C), T.qw[:, 128 * b:128 * b + 128], T.sw[:, 128 * b:128 * b + 128], T.qz[:], T.sz[:]), ["qw", "sw"] + runs("qz"), ["ps%d" % b])
+        l, k, at = (T.lk, T.lk, 18) if r else (T.glt, T.gkt, 0)
+        if r == 0:
+            differences(0)
         op("v", "scan", (T.sc2[:], hold, T.mp[:], 0.0, A.add, A.max), held + ["mp0", "mp1"], ["sc2"])
-        offsets("sc2", "ma", T["mm" + rs], "mm" + rs)
+        op("v", "tt", (T.dt2[:, 0:9], T.df[:, 0:9], T.st[:, 15:H:16], A.mult), ["df0", "st"], ["dt0"])
+        op("v", "tt", (T.dt2[:, 9:18], T.df[:, 9:18], T.st[:, 15:H:16], A.mult), ["df1", "st"], ["dt1"])
+        op("v", "ts", (T.ma[:], T.sc2[:, 7:2 * C:8], 2047, None, A.bitwise_and), ["sc2"], ["ma"])
+        op("v", "tt", (T.lk[:, 27:36], k[:, at + 9:at + 18], T.dt2[:, 0:9], A.subtract), ["dt0", "fk1"], ["fk1"])
+        op("v", "tt", (T.lk[:, 0:18], l[:, 0:18], T.dt2[:], A.add), ["fl", "dt0", "dt1"], ["fl"])
+        op("v", "tt", (T.lk[:, 18:27], k[:, at:at + 9], T.dt2[:, 9:18], A.subtract), ["dt1", "fk0"], ["fk0"])
+        op("v", "copy", (T["mm" + rs][:], T.ma[:]), ["ma"], ["mm" + rs])
         send_m(r)
-        differences(r)
         for b in range(4):
             src, dst, keys = bank(b, C), T.ht[:, b:4 * C:4], (["ps%d" % b], ["h%d" % b])
             if b == 3:
@@ -382,17 +432,15 @@ def rank_program(g, core, T, topo):
             else:
                 op("s", "act", (dst, src, F.Copy), *keys, scale=0.03125)
         hk = ["h%d" % b for b in range(4)]
-        op("v", "copy", (T.hp[:, 0:16 * HV], T.ht[:].indirect(T["mm" + rs][:, 0:HV])), hk + ["mm" + rs], ["hp0"])
-        op("s", "act", (T.hp[:, 16 * HV:576], T.ht[:].indirect(T["mm" + rs][:, HV:36]), F.Copy), hk + ["mm" + rs], ["hp1"])
+        op("v", "copy", (T.hp[:, 0:288], T.ht[:].indirect(T["mm" + rs][:, 0:18])), hk + ["mm" + rs], ["hp0"])
+        op("s", "act", (T.hp[:, 288:576], T.ht[:].indirect(T["mm" + rs][:, 18:36]), F.Copy), hk + ["mm" + rs], ["hp1"])
         op("v", "quant", (T["qh" + rs][:], T["sh" + rs][:], T.hp[:]), ["hp0", "hp1"], ["qh" + rs])
         send_h(r)
-        l, k, at = (T.lk, T.lk, 18) if r else (T.glt, T.gkt, 0)
-        op("v", "tt", (T.dt2[:, 0:9], T.df[:, 0:9], T.st[:, 15:H:16], A.mult), ["df0", "st"], ["dt0"])
-        op("v", "tt", (T.dt2[:, 9:18], T.df[:, 9:18], T.st[:, 15:H:16], A.mult), ["df1", "st"], ["dt1"])
-        op("v", "tt", (T.lk[:, 27:36], k[:, at + 9:at + 18], T.dt2[:, 0:9], A.subtract), ["dt0", "fk1"], ["fk1"])
-        op("v", "tt", (T.lk[:, 0:18], l[:, 0:18], T.dt2[:], A.add), ["fl", "dt0", "dt1"], ["fl"])
-        op("v", "tt", (T.lk[:, 18:27], k[:, at:at + 9], T.dt2[:, 9:18], A.subtract), ["dt1", "fk0"], ["fk0"])
         if r < 2:
+            for at, add, key in ((K2, 1.0, "k2"), (KE, 0.0, "ke")):
+                op("v", "ts", (T["lo%d" % (r + 1)][:, at:at + 18], T.lk[:, 18:36], 2.0, add, A.mult, A.add), ["fk0", "fk1"], ["%s_%d" % (key, r + 1)])
+            send_k(r + 1)
+            differences(r + 1)
             lists()
         else:
             op("v", "copy", (T.kf[:], T.lk[:]), ["fl", "fk0", "fk1"], ["kf"])
@@ -404,10 +452,11 @@ def rank_program(g, core, T, topo):
         if r < 2:
             scores(1)
             convert(r + 1)
-            send_k(r + 1)
             lay(1)
             sign(1)
-            factor(1, "s")
+            lifted(1)
+            factor(1)
+            signed(1)
         else:
             output(op, T, 1)
         for b in range(4):
@@ -416,10 +465,10 @@ def rank_program(g, core, T, topo):
         for b in range(4):
             op("v", "tt", (T.xt[:, b:576:4], T.xt[:, b:576:4], bank(b, H), A.add), ["ps%d" % b, "X0e%d" % b], ["X0e%d" % b])
     output(op, T, 0)
-    for sem, n in sorted(count.items()) + sorted(expect.items()):
+    g.wait_ge(T.sem["sent"], done[0])
+    for sem, n in sorted(expect.items()) + sorted(count.items(), key=lambda x: x[0] == "out"):
         if waited["g"].get(sem, 0) < n:
             g.wait_ge(T.sem[sem], n)
-    g.wait_ge(T.sem["sent"], done[0])
 
 
 def output(op, T, h):

from concourse.bass import DstId, RemoteDMATransfer
from concourse.mybir import dt, AluOpType as A, ActivationFunctionType as F

N, MASK = 8, [4, 1, 2]
C, H = 288, 144
U = 2.0 ** -118
T1 = 2048.0
TAG = T1 * U
OWN, SET, STATE = 2, 4, 40
SINK, SHIFT = 24, 24
LIFT = [1, 4, 24]
BIG = 128 * T1
RUNS = ((0, 10), (10, 18))
f32, b16, i32, u16, u8, q8 = "float32", "bfloat16", "int32", "uint16", "uint8", "float8_e4m3fn_x4"
SCRATCH = {
    "xt": ("sbuf", [128, 4 * C], b16), "ut": ("sbuf", [128, 512], b16), "vt": ("sbuf", [128, 512], b16),
    "glt": ("sbuf", [128, 18], i32), "gkt": ("sbuf", [128, 18], i32),
    "qw": ("sbuf", [128, 512], q8), "sw": ("sbuf", [128, 512], u8),
    "qu": ("sbuf", [128, 128], q8), "su": ("sbuf", [128, 128], u8),
    "qr": ("sbuf", [128, 256], q8), "sr": ("sbuf", [128, 256], u8),
    "qv": ("sbuf", [128, 128], q8), "sv": ("sbuf", [128, 128], u8),
    "qx": ("sbuf", [128, C], q8), "sx": ("sbuf", [128, C], u8),
    "qz": ("sbuf", [128, C], q8), "sz": ("sbuf", [128, C], u8),
    "qe": ("sbuf", [128, 512], q8), "se": ("sbuf", [128, 512], u8),
    "et": ("sbuf", [128, 516], b16), "ea": ("sbuf", [128, 128], f32), "cf": ("sbuf", [128, 4 * C + 2], b16),
    "pi": ("sbuf", [128, 4], i32), "pa": ("sbuf", [128, 4], i32), "pf": ("sbuf", [128, 8], f32), "up": ("sbuf", [128, 4], f32),
    "e16": ("sbuf", [128, 16], f32), "r16": ("sbuf", [128, 16], f32), "r8": ("sbuf", [128, 8], f32), "k8": ("sbuf", [128, 8], f32),
    "c16": ("sbuf", [128, H], f32), "labc": ("sbuf", [128, C], f32),
    "mask16": ("sbuf", [128, H], f32), "rs16": ("sbuf", [128, H], f32),
    "hi": ("sbuf", [128, C], f32), "own": ("sbuf", [128, C], f32), "ofi": ("sbuf", [128, 16], i32), "ofu": ("sbuf", [128, 16], u16),
    "lk": ("sbuf", [128, 36], f32), "df": ("sbuf", [128, 18], f32), "dt2": ("sbuf", [128, 18], f32),
    "lf": ("sbuf", [128, 126], f32), "kf": ("sbuf", [128, 36], u16),
    "oo": ("sbuf", [128, 72], u16), "oa": ("sbuf", [128, 72], i32), "ma": ("sbuf", [128, 72], i32),
    "sg": ("sbuf", [128, 2 * C], f32), "v0": ("sbuf", [128, 2 * C], f32), "w0": ("sbuf", [128, 2 * C], f32), "v1": ("sbuf", [128, 2 * C], f32),
    "v2": ("sbuf", [128, 3 * C], f32), "g1": ("sbuf", [128, 2 * C], f32), "g3": ("sbuf", [128, 2 * C], f32),
    "d0": ("sbuf", [128, 3 * C], f32), "d1": ("sbuf", [128, 3 * C], b16),
    "kk": ("sbuf", [128, C], f32), "nb": ("sbuf", [128, C], f32), "ow": ("sbuf", [128, C], f32),
    "sc": ("sbuf", [128, 2 * C], i32), "mp": ("sbuf", [128, 2 * C], f32), "sc2": ("sbuf", [128, 2 * C], i32),
    "mt": ("sbuf", [128, H], f32), "st": ("sbuf", [128, H], f32),
    "lrow": ("sbuf", [128, 2 * C], f32),
    "zz": ("sbuf", [128, 4 * C], b16), "zt": ("sbuf", [128, 4 * C], b16), "ht": ("sbuf", [128, 4 * C], b16), "hp": ("sbuf", [128, 4 * H], b16),
    "ys": ("sbuf", [128, C], f32),
    "ps": ("psum", [128, 4096], f32),
}
HOLD = 2 * C + 1
L2, L3, K3, K2, KE = 72, 90, 108, 126, 144
for _r in range(3):
    SCRATCH["lo%d" % _r] = ("sbuf", [128, 162], u16)
    SCRATCH["kin%d" % _r] = ("sbuf", [128, 36], u16)
    SCRATCH["mm%d" % _r] = ("sbuf", [128, 72], u16)
    SCRATCH["min%d" % _r] = ("sbuf", [128, 36], u16)
    SCRATCH["qh%d" % _r] = ("sbuf", [128, H], q8)
    SCRATCH["sh%d" % _r] = ("sbuf", [128, H], u8)
    SCRATCH["qin%d" % _r] = ("sbuf", [128, H], q8)
    SCRATCH["sin%d" % _r] = ("sbuf", [128, H], u8)
SCRATCH["hq"] = ("sbuf", [128, H // 2], q8)
SCRATCH["hs"] = ("sbuf", [128, H // 2], u8)
SCRATCH["hk"] = ("sbuf", [128, 18], u16)
SCRATCH["hm"] = ("sbuf", [128, 18], u16)
KINDS = [("hk", 36, "kin", "ak"), ("hm", 36, "min", "am"), ("hq", H, "qin", "aq"), ("hs", H, "sin", "aq")]
SEMAPHORES = ["cv", "cs", "ct", "cg", "sent", "out", "hq", "hs", "hk", "hm"] + ["%s%d" % (n, r) for n in ("ak", "am", "aq", "ga") for r in range(3)] \
    + ["ld%d" % i for i in range(8)]


def handers(topo, core, dst):
    if topo.may_write(core, dst):
        return None
    return [c for c in topo.cores_of(core) if c != core and topo.die(c) == topo.die(core) and topo.may_write(c, dst)]


def engines8(topo, src, dst):
    e = topo.engines(src, dst)[:8]
    return len(e), sum(1 << i for i in e)


def send(g, T, topo, core, dst, out, in_, sem):
    n, m = engines8(topo, core, dst)
    rid, pid = topo.addr(dst, core)
    g.remote_dma(out, in_, T.sem[sem], T.sem["sent"], pid, rid, m)
    return n


def hand_on(g, core, T, topo):
    done = 0
    for r, mask in enumerate(MASK):
        for i, a in enumerate(T.cores):
            b = T.cores[i ^ mask]
            hs = handers(topo, a, b)
            if hs is None or core not in hs:
                continue
            for kind, width, into, sem in KINDS:
                w = width // len(hs)
                c0 = hs.index(core) * w
                out, in_ = T[into + str(r)][:, c0:c0 + w], T[kind][:, 0:w]
                if kind == "hq":
                    out, in_ = out.bitcast(dt.uint8), in_.bitcast(dt.uint8)
                g.wait_ge(T.sem[kind], len(topo.engines(a, core)) // len(hs))
                done += send(g, T, topo, core, b, out, in_, sem + str(r))
    if done:
        g.wait_ge(T.sem["sent"], done)


def rank_program(g, core, T, topo):
    rank = T.rank_of(core)
    if rank is None:
        hand_on(g, core, T, topo)
        return
    Q = {"v": g.vector, "s": g.scalar, "t": g.tensor, "g": g, "y": g.sync}
    own_sem = {"v": "cv", "s": "cs", "t": "ct", "g": "cg"}
    count, waited = {}, {q: {} for q in Q}
    lastw, readers, known = {}, {}, {}

    def need(q, tok):
        sem, val, _ = tok
        if waited[q].get(sem, 0) >= val:
            return
        Q[q].wait_ge(T.sem[sem], val)
        waited[q][sem] = val
        for s, n in known.get((sem, val), {}).items():
            if waited[q].get(s, 0) < n:
                waited[q][s] = n

    def before(q, reads, writes):
        toks = [lastw[k] for k in reads + writes if k in lastw]
        toks += [t for k in writes for t in readers.get(k, []) if t[2] != q]
        best = {}
        for t in toks:
            if t[0] not in best or best[t[0]][1] < t[1]:
                best[t[0]] = t
        for t in best.values():
            need(q, t)

    def after(q, ins, sem, inc, reads, writes):
        if sem is None:
            sem = own_sem[q]
        ins.then_inc(T.sem[sem], inc)
        count[sem] = count.get(sem, 0) + inc
        tok = (sem, count[sem], q)
        known[tok[:2]] = dict(waited[q])
        for k in reads:
            readers.setdefault(k, []).append(tok)
        for k in writes:
            lastw[k] = tok
            readers[k] = []

    def parts(keys):
        return [k for key in keys for k in (["X0e%d" % b for b in range(4)] if key == "X0" else [key])]

    def op(q, name, args, reads, writes, sem=None, inc=1, **kw):
        reads, writes = parts(reads), parts(writes)
        before(q, reads, writes)
        e = Q[q]
        fn = {"copy": lambda: e.tensor_copy(*args), "tt": lambda: e.tensor_tensor(*args), "ts": lambda: e.tensor_scalar(*args),
              "scan": lambda: e.tensor_tensor_scan(*args), "quant": lambda: e.quantize_mx(*args), "memset": lambda: e.memset(*args),
              "act": lambda: e.activation(*args, **kw), "mm": lambda: e.matmul_mx(*args, True, True), "iota": lambda: e.iota(*args, **kw),
              "dma": lambda: e.dma_start(*args, **kw)}[name]
        after(q, fn(), sem, inc, reads, writes)

    def load(q, i, out, in_, key):
        op(q, "dma", (out, in_), [], [key], sem="ld%d" % i, inc=16)

    expect, done = {}, [0]

    def ship(r, kind, out, in_, width, sem, keys):
        before("g", keys, [])
        dst = T.cores[rank ^ MASK[r]]
        hs = handers(topo, core, dst)
        if hs is None:
            done[0] += send(g, T, topo, core, dst, out(slice(0, width)), in_(slice(0, width)), sem)
            return
        w, ts = width // len(hs), []
        land = T[kind][:, 0:w]
        if kind == "hq":
            land = land.bitcast(dt.uint8)
        for j, h in enumerate(hs):
            es = topo.engines(core, h)
            n = len(es) // len(hs)
            rid, pid = topo.addr(h, core)
            ts.append(RemoteDMATransfer(dst_ids=[DstId(rid=rid, pnc=pid)], dma_engine_mask=sum(1 << e for e in es[j * n:j * n + n]), remote_sem=T.sem[kind],
                                        src=in_(slice(j * w, j * w + w)), dst=land))
            done[0] += n
        g.remote_dma_fused(ts, local_sem=T.sem["sent"])

    for r in range(3):
        p = T.cores[rank ^ MASK[r]]
        n = sum(engines8(topo, c, core)[0] for c in (handers(topo, p, core) or [p]))
        for sem, times, key in (("ak", 1, "kin"), ("am", 1, "min"), ("aq", 2, "qin")):
            expect[sem + str(r)] = n * times
            lastw[key + str(r)] = (sem + str(r), n * times, "far")

    def send_k(r):
        ship(r, "hk", lambda c: T["kin%d" % r][:, c], lambda c: T["lo%d" % r][:, c.start + K2:c.stop + K2], 36, "ak%d" % r, ["k2_%d" % r, "ke_%d" % r])

    def send_m(r):
        ship(r, "hm", lambda c: T["min%d" % r][:, c], lambda c: T["mm%d" % r][:, c.start + 36:c.stop + 36], 36, "am%d" % r, ["mm%d" % r])

    def send_h(r):
        ship(r, "hq", lambda c: T["qin%d" % r][:, c].bitcast(dt.uint8), lambda c: T["qh%d" % r][:, c].bitcast(dt.uint8), H, "aq%d" % r, ["qh%d" % r])
        ship(r, "hs", lambda c: T["sin%d" % r][:, c], lambda c: T["sh%d" % r][:, c], H, "aq%d" % r, ["qh%d" % r])

    def bank(i, n):
        return T.ps[:, 512 * i:512 * i + n]

    def first(at, src, by, add, key):
        op("v", "ts", (T.lo0[:, at:at + 18], T[src][:], by, add, A.mult, A.add), [src], [key + "_0"])

    def lists():
        for t in range(4):
            op("s", "act", (T.lf[:, 18 * t:18 * t + 18], T.lk[:, 0:18], F.Copy), ["fl"], ["lf%d" % t], scale=4.0, bias=float(t))
        op("s", "act", (T.lf[:, L2:L2 + 18], T.lk[:, 0:18], F.Copy), ["fl"], ["lf4"], scale=2.0, bias=1.0)
        op("s", "act", (T.lf[:, L3:L3 + 36], T.lk[:], F.Copy), ["fl", "fk0", "fk1"], ["lf5"], scale=3.0, bias=2.0)

    def convert(r):
        op("v", "copy", (T["lo%d" % r][:, 0:K2], T.lf[:]), ["lf%d" % i for i in range(6)], ["%s_%d" % (n, r) for n in ("xl0", "xl1", "xl2", "xl3", "l2", "l3", "k3")])

    def unpacker(b):
        c = slice(128 * b, 128 * b + 128)
        op("v", "quant", (T.qe[:, c], T.se[:, c], T.et[:, 3 - b:515 - b]), ["et"], ["qe%d" % b])

    def holder(e):
        op("s", "act", (T.cf[:, HOLD + e:HOLD + 2 * C:8], T.labc[:, 0:72], F.Identity), ["labc", "k8"], ["hold%d" % e], scale=0.0, bias=T.k8[:, e:e + 1])

    hold, held = T.cf[:, HOLD:HOLD + 2 * C], ["cfz"] + ["hold%d" % e for e in range(0, 8, 2)]

    def spread(i):
        c, by = slice(128 * i, 128 * i + 128), T.ofu[:, 8 * i:8 * i + 8]
        op("v", "copy", (T.qr[:, c].bitcast(dt.uint32), T.qu[:].bitcast(dt.uint32).indirect(by)), ["qu", "ofu"], ["qr%d" % i])
        op("s", "act", (T.sr[:, c], T.su[:].indirect(by), F.Copy), ["qu", "ofu"], ["sr%d" % i])

    def scores(h):
        c, e = slice(H * h, H * h + H), slice(4 * H * h, 4 * H * h + 4 * H)
        n = "ab"[h]
        op("v", "quant", (T.qx[:, c], T.sx[:, c], T.xt[:, e]), ["X%d" % h], ["qx" + n])
        op("t", "mm", (bank(4 + h, H), T.qr[:, 0:128], T.sr[:, 0:128], T.qx[:, c], T.sx[:, c]), ["qr0", "sr0", "qx" + n], ["ps%d" % (4 + h)])

    def span(h, n, at):
        a, b = ((0, H), (H, C), (0, C))[h]
        return slice(n * a + at, n * b, n)

    def names(key, h):
        return [key + n for n in ("a", "b", "ab")[h]]

    def runs(key):
        return ["%s%d" % (key, a) for a, b in RUNS]

    def lay(h):
        op("v", "tt", (T.v0[:, span(h, 2, 1)], bank(4 + h, H), T.hi[:, span(h, 1, 0)], A.min), ["ps%d" % (4 + h), "hi", "v0z"], names("V0", h) + ["V0c"])

    def sign(h):
        op("v", "ts", (T.sg[:, span(h, 2, 1)], bank(4 + h, H), 0.0, 0.5, A.is_gt, A.subtract), ["ps%d" % (4 + h), "sgz"], names("sg", h))

    def lifted(h):
        op("s", "act", (T.w0[:, span(h, 2, 1)], T.v0[:, span(h, 2, 1)], F.Copy), names("V0", h), names("w0", h), bias=LIFT[0] * TAG)

    def factor(h):
        op("s", "act", (T.cf[:, span(h, 2, 1)], T.sg[:, span(h, 2, 1)], F.Copy), names("sg", h), names("i1", h), scale=-4.0 * STATE * TAG)

    def signed(h):
        op("s", "act", (T.d0[:, span(h, 3, 1)], T.sg[:, span(h, 2, 1)], F.Copy), names("sg", h) + ["up"], names("d0", h), scale=T.up[:, 2:3])

    def xl(r, t, q):
        out, in_, keys = T.zz[:, t:4 * C:4], T.xt[:].indirect(T["lo%d" % r][:, 18 * t:18 * t + 18]), (["X0", "X1", "xl%d_%d" % (t, r)], ["zz%d" % t])
        if q == "s":
            op("s", "act", (out, in_, F.Copy), *keys)
        else:
            op("v", "copy", (out, in_), *keys)

    zk = ["zz%d" % t for t in range(4)]

    def add_x(r):
        op("g", "dma", (T.zz[:], T.xt[:]), ["X0", "X1"] + zk, zk, sem="ga%d" % r, inc=16, accum_op=A.add)

    def differences(r):
        l, k = (T.lk, T.lk) if r else (T.glt, T.gkt)
        at = 18 if r else 0
        op("v", "tt", (T.df[:, 0:9], k[:, at + 9:at + 18], l[:, 0:9], A.subtract), ["fl", "fk1", "glt", "gkt"], ["df0"])
        op("v", "tt", (T.df[:, 9:18], k[:, at:at + 9], l[:, 9:18], A.subtract), ["fl", "fk0", "glt", "gkt"], ["df1"])

    imprecise = {"allow_small_or_imprecise_dtypes": True}
    load("y", 0, T.gkt[:], T.gk[:], "gkt")
    load("s", 1, T.glt[:], T.gl[:], "glt")
    load("s", 2, T.ut[:], T.u[:], "ut")
    load("y", 3, T.xt[:, 576:1152], T.x[:, 576:1152], "X1")
    load("y", 4, T.xt[:, 0:576], T.x[:, 0:576], "X0")
    before("y", parts(["X0", "X1"]), [])
    load("y", 5, T.qw[:].bitcast(dt.uint8), T.wc[:], "qw")
    load("y", 6, T.vt[:], T.v[:], "vt")
    op("g", "iota", (T.pi[:], [[0, 4]], 0, 1), [], ["pi"])
    op("g", "iota", (T.e16[:], [[0, 2], [1, 8]], 0, 0), [], ["e16"], **imprecise)
    op("g", "iota", (T.labc[:], [[4, C]], 0, 0), [], ["labc"], **imprecise)
    op("g", "iota", (T.ofi[:], [[1, 2], [16, 8]], 0, 0), [], ["ofi"])
    op("g", "iota", (T.c16[:], [[0, 9], [1, 16]], 0, 0), [], ["c16"], **imprecise)
    op("g", "iota", (T.v0[:, 0:2 * C:2], [[0, C]], 0, 0), [], ["v0z"], **imprecise)
    op("g", "iota", (T.w0[:, 0:2 * C:2], [[0, C]], 0, 0), [], ["w0z"], **imprecise)
    op("g", "iota", (T.d0[:, 0:3 * C:3], [[0, C]], 0, 0), [], ["d0z"], **imprecise)
    load("g", 7, T.sw[:], T.ws[:], "sw")
    op("v", "memset", (T.et[:], 0.0), [], ["et"])
    op("v", "ts", (T.pa[:, 1:2], T.pi[:, 1:2], 3, None, A.bitwise_and), ["pi"], ["pa1"])
    op("v", "ts", (T.pa[:, 2:3], T.pi[:, 2:3], 12, 1, A.bitwise_and, A.logical_shift_right), ["pi"], ["pa2"])
    op("v", "ts", (T.pa[:, 0:1], T.pi[:, 0:1], 15, None, A.bitwise_and), ["pi"], ["pa0"])
    op("v", "ts", (T.pf[:, 4:5], T.pa[:, 1:2], U, SET * TAG, A.mult, A.add), ["pa1"], ["pf4"])
    op("v", "ts", (T.pf[:, 3:4], T.pi[:, 3:4], -4.0, None, A.mult), ["pi"], ["pf3"])
    op("v", "copy", (T.pf[:, 0:3], T.pa[:, 0:3]), ["pa0", "pa1", "pa2"], ["pf"])
    op("v", "memset", (T.cf[:, 0:HOLD + 2 * C:2], 0.0), [], ["cfz"])
    op("v", "memset", (T.sg[:, 0:2 * C:2], 0.0), [], ["sgz"])
    op("v", "ts", (T.r16[:], T.e16[:], T.pf[:, 2:3], BIG, A.is_equal, A.mult), ["e16", "pf"], ["r16"])
    op("v", "ts", (T.up[:], T.e16[:, 0:4], 2.0 ** 59, 2.0 ** 59, A.mult, A.mult), ["e16"], ["up"])
    op("v", "copy", (T.ofu[:], T.ofi[:]), ["ofi"], ["ofu"])
    op("v", "ts", (T.r8[:], T.r16[:, 8:16], -2.0, None, A.mult), ["r16"], ["r8"])
    op("v", "ts", (T.mask16[:], T.c16[:], T.pf[:, 0:1], -1e28, A.not_equal, A.mult), ["c16", "pf"], ["mask16"])
    op("v", "tt", (T.k8[:], T.r8[:], T.r16[:, 6:14], A.add), ["r8", "r16"], ["k8"])
    op("s", "act", (T.d1[:, 1:3 * C:3], T.et[:, 0:C], F.Copy), ["et"], ["d1z"])
    op("s", "act", (T.d1[:, 2:3 * C:3], T.et[:, 0:C], F.Copy), ["et"], ["d1s"], bias=SHIFT * T1)
    op("s", "act", (T.hi[:], T.labc[:], F.Identity), ["labc", "pf4"], ["hi"], scale=U, bias=T.pf[:, 4:5])
    op("s", "act", (T.ea[:], T.labc[:, 0:128], F.Abs), ["labc", "pf3"], ["ea"], bias=T.pf[:, 3:4])
    op("s", "act", (T.own[:], T.hi[:], F.Copy), ["hi"], ["own"], bias=(OWN - SET) * TAG)
    op("s", "act", (T.et[:, 3:515:4], T.ea[:], F.Relu), ["ea", "d1z", "d1s"], ["et"], scale=-1.0, bias=1.0)
    op("s", "act", (T.rs16[:], T.c16[:], F.Sign), ["c16"], ["rs16"])
    for t in range(4):
        first(18 * t, "glt", 4.0, float(t), "xl%d" % t)
    holder(0)
    holder(2)
    op("v", "quant", (T.qu[:], T.su[:], T.ut[:]), ["ut"], ["qu"])
    first(K2, "gkt", 2.0, 1.0, "k2")
    spread(0)
    scores(1)
    first(KE, "gkt", 2.0, 0.0, "ke")
    send_k(0)
    first(L2, "glt", 2.0, 1.0, "l2")
    for r in range(3):
        rs = str(r)
        lo = T["lo" + rs]
        late = 0 if r else 2
        wk, sk = ["V0a", "V0b", "V0c", "v0z"], ["sga", "sgb", "sgz"]
        scores(0)
        if r == 0:
            lay(1)
            sign(1)
        xl(r, 0, "s")
        xl(r, 1, "s")
        if r:
            xl(r, 3, "v")
        sign(0)
        lay(0)
        op("v", "tt", (T.kk[:], T.v0[:].indirect(lo[:, K2:K2 + 18]), T.own[:], A.max), wk + ["k2_" + rs, "own"], runs("kk"))
        op("s", "act", (T.nb[:], T.sg[:].indirect(lo[:, K2:K2 + 18]), F.Copy), sk + ["k2_" + rs], ["nb"], scale=-1.0)
        lifted(late)
        if r:
            xl(r, 2, "s")
            add_x(r)
            factor(late)
            signed(late)
        else:
            factor(late)
            xl(r, 2, "s")
            xl(r, 3, "s")
            add_x(r)
        op("v", "tt", (T.g1[:, 0:2 * C:2], T.sg[:].indirect(lo[:, L2:L2 + 18]), T.nb[:], A.min), sk + ["l2_" + rs, "nb"], ["s1"])
        for a, b in RUNS:
            op("v", "tt", (T.g1[:, 32 * a + 1:32 * b:2], T.w0[:].indirect(lo[:, L2 + a:L2 + b]), T.kk[:, 16 * a:16 * b], A.max),
               ["kk%d" % a, "w0a", "w0b", "w0z", "l2_" + rs], ["m1%d" % a])
        op("s", "act", (T.ow[:], T.g1[:, 1:2 * C:2], F.Copy), runs("m1"), ["ow"], scale=-1.0, bias=-SINK * TAG)
        if r == 0:
            signed(late)
        for a, b in RUNS:
            e, odd = slice(32 * a, 32 * b), slice(32 * a + 1, 32 * b, 2)
            op("v", "scan", (T.v1[:, e], T.cf[:, e], T.g1[:, e], 0.0, A.mult, A.add), ["i1a", "i1b", "cfz", "s1", "m1%d" % a], ["V1%d" % a])
            op("s", "act", (T.v0[:, odd], T.v1[:, odd], F.Copy), ["V1%d" % a], ["V0c"] if a else ["V0a", "V0b"], bias=LIFT[1] * TAG)
        if r == 0:
            first(L3, "glt", 3.0, 2.0, "l3")
            spread(1)
        op("t", "mm", (bank(6, H), T.qr[:, 128:256], T.sr[:, 128:256], T.qx[:, 0:H], T.sx[:, 0:H]), ["qr1", "sr1", "qxa"], ["ps6"])
        for a, b in RUNS:
            c = slice(16 * a, 16 * b)
            op("v", "tt", (T.kk[:, c], T.v1[:].indirect(lo[:, K2 + a:K2 + b]), T.ow[:, c], A.max), runs("V1") + ["k2_" + rs, "ow"], ["kk%d" % a])
            op("s", "act", (T.d1[:, 48 * a:48 * b:3], T.kk[:, c], F.Sign), ["kk%d" % a], ["b1%d" % a])
        for a, b in RUNS:
            op("v", "tt", (T.d0[:, 48 * a + 2:48 * b:3], T.v0[:].indirect(lo[:, L2 + a:L2 + b]), T.kk[:, 16 * a:16 * b], A.max), wk + ["l2_" + rs, "kk%d" % a], ["mx%d" % a])
        if r == 0:
            first(K3, "gkt", 3.0, 2.0, "k3")
        op("s", "act", (T.ow[:], T.d0[:, 2:3 * C:3], F.Abs), runs("mx") + ["up"], ["ow"], scale=T.up[:, 1:2])
        for a, b in RUNS:
            e = slice(48 * a, 48 * b)
            op("v", "scan", (T.v2[:, e], T.d0[:, e], T.d1[:, e], 0.0, A.mult, A.add), ["d0z", "d0a", "d0b", "mx%d" % a, "d1z", "d1s", "b1%d" % a], ["V2%d" % a])
        if r == 0:
            holder(4)
            holder(6)
            unpacker(0)
        op("v", "tt", (T.mt[:], bank(6, H), T.mask16[:], A.is_lt), ["ps6", "mask16"], ["mt"])
        for a, b in RUNS:
            op("v", "tt", (T.g3[:, 32 * a:32 * b:2], T.v2[:].indirect(lo[:, K3 + a:K3 + b]), T.ow[:, 16 * a:16 * b], A.max), runs("V2") + ["k3_" + rs, "ow"], ["kk3%d" % a])
            op("s", "act", (T.g3[:, 32 * a + 1:32 * b:2], T.v2[:].indirect(lo[:, L3 + a:L3 + b]), F.Copy), runs("V2") + ["l3_" + rs], ["gg3%d" % a], bias=LIFT[2] * T1)
        for a, b in RUNS:
            op("v", "scan", (T.sc[:, 32 * a:32 * b], T.cf[:, HOLD + 32 * a:HOLD + 32 * b], T.g3[:, 32 * a:32 * b], 0.0, A.add, A.max), held + ["kk3%d" % a, "gg3%d" % a], ["sc%d" % a])
        gk = runs("kk3") + runs("gg3") + ["kin" + rs]
        op("s", "act", (T.mp[:, 1:2 * C:2], T.g3[:].indirect(T["kin" + rs][:, 0:18]), F.Copy), gk, ["mp1"])
        for a, b in RUNS:
            op("v", "ts", (T.oa[:, 4 * a:4 * b], T.sc[:, 32 * a + 7:32 * b:8], 2047, None, A.bitwise_and), ["sc%d" % a], ["oa%d" % a])
            if r == 0 and a == 0:
                unpacker(1)
        op("v", "scan", (T.st[:], T.rs16[:], T.mt[:], 0.0, A.mult, A.add), ["rs16", "mt"], ["st"])
        for a, b in RUNS:
            op("v", "copy", (T.oo[:, 4 * a:4 * b], T.oa[:, 4 * a:4 * b]), ["oa%d" % a], ["oo%d" % a])
            if r == 0 and a == 0:
                unpacker(2)
        (a, b), (c, d) = RUNS
        op("s", "act", (T.zt[:, 64 * a:64 * b], T.zz[:].indirect(T.oo[:, 4 * a:4 * b]), F.Copy), zk + ["oo%d" % a], ["zt%d" % a], scale=0.5)
        op("v", "ts", (T.zt[:, 64 * c:64 * d], T.zz[:].indirect(T.oo[:, 4 * c:4 * d]), 0.5, None, A.mult), zk + ["oo%d" % c], ["zt%d" % c])
        op("s", "act", (T.mp[:, 0:2 * C:2], T.g3[:].indirect(T["kin" + rs][:, 18:36]), F.Copy), gk, ["mp0"])
        if r == 0:
            unpacker(3)
        for a, b in RUNS[::-1]:
            op("v", "quant", (T.qz[:, 16 * a:16 * b], T.sz[:, 16 * a:16 * b], T.zt[:, 64 * a:64 * b]), ["zt%d" % a], ["qz%d" % a])
        for b in range(4):
            op("t", "mm", (bank(b, C), T.qw[:, 128 * b:128 * b + 128], T.sw[:, 128 * b:128 * b + 128], T.qz[:], T.sz[:]), ["qw", "sw"] + runs("qz"), ["ps%d" % b])
        l, k, at = (T.lk, T.lk, 18) if r else (T.glt, T.gkt, 0)
        if r == 0:
            differences(0)
        op("v", "scan", (T.sc2[:], hold, T.mp[:], 0.0, A.add, A.max), held + ["mp0", "mp1"], ["sc2"])
        op("v", "tt", (T.dt2[:, 0:9], T.df[:, 0:9], T.st[:, 15:H:16], A.mult), ["df0", "st"], ["dt0"])
        op("v", "tt", (T.dt2[:, 9:18], T.df[:, 9:18], T.st[:, 15:H:16], A.mult), ["df1", "st"], ["dt1"])
        op("v", "ts", (T.ma[:], T.sc2[:, 7:2 * C:8], 2047, None, A.bitwise_and), ["sc2"], ["ma"])
        op("v", "tt", (T.lk[:, 27:36], k[:, at + 9:at + 18], T.dt2[:, 0:9], A.subtract), ["dt0", "fk1"], ["fk1"])
        op("v", "tt", (T.lk[:, 0:18], l[:, 0:18], T.dt2[:], A.add), ["fl", "dt0", "dt1"], ["fl"])
        op("v", "tt", (T.lk[:, 18:27], k[:, at:at + 9], T.dt2[:, 9:18], A.subtract), ["dt1", "fk0"], ["fk0"])
        op("v", "copy", (T["mm" + rs][:], T.ma[:]), ["ma"], ["mm" + rs])
        send_m(r)
        for b in range(4):
            src, dst, keys = bank(b, C), T.ht[:, b:4 * C:4], (["ps%d" % b], ["h%d" % b])
            if b == 3:
                op("v", "ts", (dst, src, 0.03125, None, A.mult), *keys)
            else:
                op("s", "act", (dst, src, F.Copy), *keys, scale=0.03125)
        hk = ["h%d" % b for b in range(4)]
        op("v", "copy", (T.hp[:, 0:288], T.ht[:].indirect(T["mm" + rs][:, 0:18])), hk + ["mm" + rs], ["hp0"])
        op("s", "act", (T.hp[:, 288:576], T.ht[:].indirect(T["mm" + rs][:, 18:36]), F.Copy), hk + ["mm" + rs], ["hp1"])
        op("v", "quant", (T["qh" + rs][:], T["sh" + rs][:], T.hp[:]), ["hp0", "hp1"], ["qh" + rs])
        send_h(r)
        if r < 2:
            for at, add, key in ((K2, 1.0, "k2"), (KE, 0.0, "ke")):
                op("v", "ts", (T["lo%d" % (r + 1)][:, at:at + 18], T.lk[:, 18:36], 2.0, add, A.mult, A.add), ["fk0", "fk1"], ["%s_%d" % (key, r + 1)])
            send_k(r + 1)
            differences(r + 1)
            lists()
        else:
            op("v", "copy", (T.kf[:], T.lk[:]), ["fl", "fk0", "fk1"], ["kf"])
            op("s", "act", (T.lrow[:], T.labc[:].indirect(T.kf[:]), F.Copy), ["labc", "kf"], ["lrow"], scale=0.25)
            op("y", "dma", (T.lr[:], T.lrow[0:128:16, :]), ["lrow"], ["lr"], sem="out", inc=16)
        if r == 1:
            op("v", "quant", (T.qv[:], T.sv[:], T.vt[:]), ["vt"], ["qv"])
        op("v", "tt", (T.xt[:, 576:1152], T.ht[:].indirect(T["min" + rs][:]), T.xt[:, 576:1152], A.add), hk + ["min" + rs, "X1"], ["X1"])
        if r < 2:
            scores(1)
            convert(r + 1)
            lay(1)
            sign(1)
            lifted(1)
            factor(1)
            signed(1)
        else:
            output(op, T, 1)
        for b in range(4):
            op("t", "mm", (bank(b, H), T.qe[:, 128 * b:128 * b + 128], T.se[:, 128 * b:128 * b + 128], T["qin" + rs][:], T["sin" + rs][:]),
               ["qe%d" % b, "qin" + rs], ["ps%d" % b])
        for b in range(4):
            op("v", "tt", (T.xt[:, b:576:4], T.xt[:, b:576:4], bank(b, H), A.add), ["ps%d" % b, "X0e%d" % b], ["X0e%d" % b])
    output(op, T, 0)
    g.wait_ge(T.sem["sent"], done[0])
    for sem, n in sorted(expect.items()) + sorted(count.items(), key=lambda x: x[0] == "out"):
        if waited["g"].get(sem, 0) < n:
            g.wait_ge(T.sem[sem], n)


def output(op, T, h):
    n, c, e, at = "ab"[h], slice(H * h, H * h + H), slice(4 * H * h, 4 * H * h + 4 * H), 512 * (4 + h)
    op("v", "quant", (T.qx[:, c], T.sx[:, c], T.xt[:, e]), ["X%d" % h], ["qx" + n])
    op("t", "mm", (T.ps[:, at:at + H], T.qv[:], T.sv[:], T.qx[:, c], T.sx[:, c]), ["qv", "qx" + n], ["ps%d" % (4 + h)])
    op("y", "dma", (T.oc[:, e], T.qx[:, c].bitcast(dt.uint8)), ["qx" + n], ["oc" + n], sem="out", inc=16)
    for k in range(4):
        op("ys"[k // 2], "dma", (T.osc[4 * k:4 * k + 4, c], T.sx[32 * k:32 * k + 4, c]), ["qx" + n], ["osc%s%d" % (n, k)], sem="out", inc=16)
    op("v", "copy", (T.ys[:, c], T.ps[:, at:at + H]), ["ps%d" % (4 + h)], ["ys" + n])
    op("s", "dma", (T.y[:, c], T.ys[:, c]), ["ys" + n], ["y" + n], sem="out", inc=16)
